import numpy as np
import ml_dtypes


def mxq(x, axis, fmt="e4m3"):
    dtype, down = {"e4m3": (ml_dtypes.float8_e4m3fn, 7), "e5m2": (ml_dtypes.float8_e5m2, 14)}[fmt]
    v = np.moveaxis(np.asarray(x, np.float32).astype(ml_dtypes.bfloat16).astype(np.float64), axis, -1)
    blocks = v.reshape(v.shape[:-1] + (-1, 32))
    amax = np.abs(blocks).max(-1, keepdims=True)
    byte = np.maximum(np.where(amax > 0, np.frexp(amax)[1] - 1 + 127, 0) - down, 1)
    scale = np.exp2(byte - 127.0)
    codes = (blocks / scale).astype(np.float32).astype(dtype).astype(np.float64)
    return np.moveaxis((codes * scale).reshape(v.shape), -1, axis)


WIDE = False


def mx_kscale(k):
    if not WIDE:
        return np.ones(k)
    levels = np.array([10, -10, 5, -5, 0])
    if k % 512:
        return np.exp2(np.random.permutation(np.resize(levels, k // 32))).repeat(32)
    a = np.empty((k // 512, 16))
    for p in range(k // 512):
        a[p, :8] = np.random.permutation(np.resize(levels, 8))
        for g in range(8):
            far = levels[np.abs(levels - a[p, g]) >= 10]
            a[p, g + 8] = far[np.random.randint(len(far))]
    return np.exp2(a.ravel()).repeat(32)


def f64(x):
    return np.asarray(x).astype(np.float64)


def striped(idx):
    return np.tile(idx.reshape(-1, 16).T, (8, 1)).astype(np.uint16)


def unstriped(offs):
    return offs[:16].T.reshape(-1).astype(np.int64)


E2M1 = np.array([0.0, 0.5, 1.0, 1.5, 2.0, 3.0, 4.0, 6.0, -0.0, -0.5, -1.0, -1.5, -2.0, -3.0, -4.0, -6.0])


def pack_fp4(w):
    k, n = w.shape
    w = f64(np.asarray(w, np.float32).astype(ml_dtypes.bfloat16)).reshape(k // 32, 32, n)
    amax = np.abs(w).max(1)
    mant, ex = np.frexp(amax / 6.0)
    byte = np.clip(np.where(amax > 0, np.where(mant > 0.5, ex, ex - 1) + 127, 1), 1, 254)
    scaled = (w * np.exp2(127.0 - byte)[:, None, :]).reshape(k, n).astype(np.float32)
    c = np.ascontiguousarray(scaled.reshape(k // 512, 128, 4, n).transpose(0, 1, 3, 2)).astype(ml_dtypes.float4_e2m1fn).view(np.uint8) & 0xF
    words = (c[..., 0::2] | (c[..., 1::2] << 4)).reshape(k // 512, 128, 2 * n)
    return np.ascontiguousarray(words), np.ascontiguousarray(byte.astype(np.uint8).reshape(k // 512, 16, n))


def unpack_fp4(words, scales):
    g, _, n = scales.shape
    words = np.ascontiguousarray(words).reshape(g, 128, n, 2)
    nib = np.empty((g, 128, n, 4), np.uint8)
    nib[..., 0::2] = words & 0xF
    nib[..., 1::2] = words >> 4
    vals = E2M1[nib] * np.repeat(np.exp2(scales.astype(np.float64) - 127.0), 8, axis=1)[..., None]
    return vals.transpose(0, 1, 3, 2).reshape(g * 512, n)


K, T, S, D, V, N = 512, 4096, 1024, 3, 512, 256
P = 2 ** 7


def setup_inputs():
    n = np.random.standard_normal
    s = mx_kscale(K)[:, None]
    packed_w1 = pack_fp4(n((K, N)) / np.sqrt(K) / s)
    return {
        "xT": (n((K, T)) * s).astype(np.float32),
        "w1_words": packed_w1[0],
        "w1_scales": packed_w1[1],
        "gate": (np.tile(np.random.uniform(0.2, 1.0, (D, 1, V)) / np.sqrt(D), (1, P, 1))).astype(np.float32),
        "offs": striped(np.random.permutation(T)[:S]),
        "cen": striped(np.random.permutation(S)[:V]),
        "pos1": striped(np.random.permutation(S)[:V]),
        "pos2": striped(np.random.permutation(S)[:V]),
        "pos3": striped(np.random.permutation(S)[:V]),
    }


def reference(xT, w1_words, w1_scales, gate, offs, cen, pos1, pos2, pos3):
    xq = mxq(f64(xT)[:, unstriped(offs)], 0, "e4m3")
    y = unpack_fp4(w1_words, w1_scales).T @ xq
    yc = y[:, unstriped(cen)]
    return yc + (y[:, unstriped(pos1)] - yc) * f64(gate)[0, :1] + (y[:, unstriped(pos2)] - yc) * f64(gate)[1, :1] + (y[:, unstriped(pos3)] - yc) * f64(gate)[2, :1]

@@ -1,0 +1,196 @@
+from contextlib import ExitStack
+
+import concourse.mybir as mybir
+from concourse.masks import make_identity
+
+K, T, S, D, V, N = 512, 4096, 1024, 3, 512, 256
+FLOPS = 2 * K * N * S
+
+F32 = mybir.dt.float32
+BF16 = mybir.dt.bfloat16
+I32 = mybir.dt.int32
+U32 = mybir.dt.uint32
+U16 = mybir.dt.uint16
+U8 = mybir.dt.uint8
+FP8X4 = mybir.dt.float8_e4m3fn_x4
+FP4X4 = mybir.dt.float4_e2m1fn_x4
+COPY = mybir.ActivationFunctionType.Copy
+MULT = mybir.AluOpType.mult
+ADD = mybir.AluOpType.add
+
+P = 128
+PACK = 4
+HALF = S // 2
+QUARTER = S // 4
+LIST = 16
+VT = V // P
+LAST_PLANE_CHUNKS = (1024, 1024, 1024, 768, 256)
+
+
+def tile_picked_grand_none_e_kernel(
+    tc, xT, w1_words, w1_scales, gate, offs, cen, pos1, pos2, pos3, out
+):
+    nc = tc.nc
+    with ExitStack() as ctx:
+        keep = ctx.enter_context(tc.tile_pool(name="keep", bufs=1))
+        ring = ctx.enter_context(tc.tile_pool(name="ring", bufs=4))
+        psum = ctx.enter_context(tc.psum_pool(name="psum", bufs=1))
+
+        offs_sb = keep.tile([P, S // LIST], U16, name="offs_sb")
+        lists = [keep.tile([P, V // LIST], U16, name="list%d" % i) for i in range(D + 1)]
+
+        w_scale = keep.tile([P, N], U8, name="w_scale", align_bytes=64)
+        gate_rows = keep.tile([P, P], F32, name="gate_rows")
+        ident = keep.tile([P, P], F32, name="ident")
+        nc.vector.memset(gate_rows[:], 0.0)
+        nc.vector.memset(w_scale[:].bitcast(I32), 0)
+        make_identity(nc, ident[:])
+
+        rows = xT.rearrange("(p j) t -> p j t", j=PACK)
+        planes = [keep.tile([P, T], F32, name="plane%d" % j) for j in range(PACK)]
+        nc.sync.dma_start(out=planes[0][:], in_=rows[:, 0, :])
+        nc.sync.dma_start(offs_sb[:], offs)
+        gate_flat = gate.rearrange("d r (t p) -> (d r t) p", p=P)
+        stride = P + 1
+        nc.sync.dma_start(out=gate_rows[0 : D * VT, :], in_=gate_flat[0 : (D * VT - 1) * stride + 1 : stride, :])
+        for j in range(1, PACK - 1):
+            nc.sync.dma_start(out=planes[j][:], in_=rows[:, j, :])
+        chunks = []
+        c0 = 0
+        for width in LAST_PLANE_CHUNKS:
+            chunks.append(slice(c0, c0 + width))
+            c0 = c0 + width
+        for cols in chunks:
+            nc.sync.dma_start(out=planes[PACK - 1][:, cols], in_=rows[:, PACK - 1, cols])
+        w_codes = keep.tile([P, 2 * N], U8, name="w_codes", align_bytes=64)
+        nc.sync.dma_start(out=w_codes[:], in_=w1_words[0])
+        for q in range(4):
+            nc.sync.dma_start(
+                out=w_scale[32 * q : 32 * q + 4, :].bitcast(I32), in_=w1_scales[0, 4 * q : 4 * q + 4, :].bitcast(I32)
+            )
+        for tile_, src in zip(lists, (cen, pos1, pos2, pos3)):
+            nc.sync.dma_start(tile_[:], src)
+        last_gate = keep.tile([P, V], F32, name="last_gate")
+        nc.sync.dma_start(out=last_gate[:], in_=gate[D - 1])
+
+
+        gate_t = psum.tile([P, V], F32, name="gate_t", tag="bank4")
+        nc.tensor.transpose(gate_t[:, 0:P], gate_rows[:], ident[:])
+        factor = keep.tile([P, (D + 1) * VT], F32, name="factor")
+        gate_sum = keep.tile([P, VT], F32, name="gate_sum")
+        nc.vector.tensor_copy(out=factor[:, VT:], in_=gate_t[:, 0 : D * VT])
+        nc.vector.tensor_reduce(
+            out=gate_sum[:], in_=gate_t[:, 0 : D * VT].rearrange("p (d t) -> p t d", d=D), axis=mybir.AxisListType.X, op=ADD
+        )
+        nc.vector.tensor_scalar(out=factor[:, 0:VT], in0=gate_sum[:], scalar1=-1.0, scalar2=1.0, op0=MULT, op1=ADD)
+
+        grouped = [keep.tile([P, HALF, PACK], BF16, name="grouped%d" % h, align_bytes=64) for h in range(2)]
+        half_offs = [offs_sb[:, h * HALF // LIST : (h + 1) * HALF // LIST] for h in range(2)]
+        for j in range(PACK - 1):
+            for h in range(2):
+                nc.vector.tensor_copy(out=grouped[h][:, :, j], in_=planes[j][:].indirect(half_offs[h]))
+        last_bf = keep.tile([P, T], BF16, name="last_bf")
+        for i, cols in enumerate(chunks):
+            if i == 3:
+                nc.vector.tensor_copy(out=last_bf[:, cols], in_=planes[PACK - 1][:, cols])
+            else:
+                nc.scalar.activation(out=last_bf[:, cols], in_=planes[PACK - 1][:, cols], func=COPY)
+        nc.vector.tensor_copy(out=grouped[1][:, :, PACK - 1], in_=planes[PACK - 1][:].indirect(half_offs[1]))
+        nc.scalar.activation(out=grouped[0][:, :, PACK - 1], in_=last_bf[:].indirect(half_offs[0]), func=COPY)
+
+        codes = [keep.tile([P, HALF], U32, name="codes%d" % h, align_bytes=64) for h in range(2)]
+        scales = [keep.tile([P, HALF], U8, name="scales%d" % h, align_bytes=64) for h in range(2)]
+        y = [keep.tile([P, S], F32, name="y%d" % b) for b in range(2)]
+
+        def product(b, h, cols, last, bank):
+            acc = psum.tile([P, V], F32, name="acc", tag="bank%d" % bank)
+            width = cols.stop - cols.start
+            nc.tensor.matmul_mx(
+                out=acc[:, 0:width],
+                lhsT=w_codes[:, 2 * P * b : 2 * P * (b + 1)].bitcast(FP4X4),
+                lhsT_scale=w_scale[:, P * b : P * (b + 1)],
+                rhs=codes[h][:, cols].bitcast(FP8X4),
+                rhs_scale=scales[h][:, cols],
+                start=True,
+                stop=True,
+            )
+            dst = y[b][:, h * HALF + cols.start : h * HALF + cols.stop]
+            if last:
+                nc.vector.tensor_copy(out=dst, in_=acc[:, 0:width])
+            else:
+                nc.scalar.activation(out=dst, in_=acc[:, 0:width], func=COPY)
+
+        for h in (1, 0):
+            flat = grouped[h][:].rearrange("p n j -> p (n j)")
+            for u in range(2):
+                cols = slice(u * QUARTER, (u + 1) * QUARTER)
+                nc.vector.quantize_mx(
+                    out=codes[h][:, cols].bitcast(FP8X4),
+                    scales=scales[h][:, cols],
+                    in_=flat[:, PACK * cols.start : PACK * cols.stop],
+                )
+                product(0, h, cols, h == 0 and u == 1, 2 * (1 - h) + u)
+        for h in (1, 0):
+            product(1, h, slice(0, HALF), False, 2 + h)
+
+        turns = []
+
+        def turned_term(b, d, cols, total, first, final):
+            width = cols.stop - cols.start
+            tiles = width // P
+            picked = ring.tile([P, width], F32, name="picked", tag="picked")
+            nc.vector.tensor_copy(
+                out=picked[:], in_=y[b][:].indirect(lists[d][:, cols.start // LIST : cols.stop // LIST])
+            )
+            turned = psum.tile([P, V], F32, name="turned", tag="bank%d" % ((4 + len(turns)) % 5))
+            turns.append(b)
+            for t in range(tiles):
+                nc.tensor.transpose(turned[:, t * P : (t + 1) * P], picked[:, t * P : (t + 1) * P], ident[:])
+            weighted = ring.tile([P, width], F32, name="weighted", tag="weighted")
+            for t in range(tiles):
+                col = d * VT + cols.start // P + t
+                nc.scalar.activation(
+                    out=weighted[:, t * P : (t + 1) * P],
+                    in_=turned[:, t * P : (t + 1) * P],
+                    func=COPY,
+                    scale=factor[:, col : col + 1],
+                )
+            for t in range(tiles):
+                vt = cols.start // P + t
+                bank, at = total(vt)
+                nc.tensor.matmul(
+                    bank[:, at * P : (at + 1) * P],
+                    lhsT=weighted[:, t * P : (t + 1) * P],
+                    rhs=ident[:],
+                    is_transpose=True,
+                    start=first and at == 0,
+                    stop=final(vt),
+                )
+
+        whole = slice(0, V)
+        total0 = psum.tile([P, V], F32, name="total0")
+        for d in range(D + 1):
+            turned_term(0, d, whole, lambda vt: (total0, vt), d == 0, lambda vt: d == D and vt == VT - 1)
+        result0 = keep.tile([P, V], F32, name="result0")
+        nc.scalar.activation(out=result0[:], in_=total0[:], func=COPY)
+        nc.sync.dma_start(out=out[0:P, :], in_=result0[:])
+
+        total1 = [psum.tile([P, V], F32, name="total1_%d" % u) for u in range(2)]
+        for d in range(D):
+            pieces = [whole] if d < D - 1 else [slice(0, V // 2), slice(V // 2, V)]
+            for cols in pieces:
+                turned_term(
+                    1, d, cols, lambda vt: (total1[vt // 2], vt % 2), d == 0, lambda vt: d == D - 1 and vt % 2 == 1
+                )
+        for u in range(2):
+            cols = slice(u * V // 2, (u + 1) * V // 2)
+            pulled = keep.tile([P, V // 2], F32, name="pulled%d" % u)
+            nc.vector.tensor_tensor(
+                out=pulled[:],
+                in0=y[1][:].indirect(lists[D][:, cols.start // LIST : cols.stop // LIST]),
+                in1=last_gate[:, cols],
+                op=MULT,
+            )
+            result1 = keep.tile([P, V // 2], F32, name="result1_%d" % u)
+            nc.vector.tensor_tensor(out=result1[:], in0=total1[u][:, 0 : V // 2], in1=pulled[:], op=ADD)
+            nc.sync.dma_start(out=out[P : 2 * P, cols], in_=result1[:])

@@ -70,8 +70,6 @@ def tile_picked_grand_none_e_kernel(
             )
         for tile_, src in zip(lists, (cen, pos1, pos2, pos3)):
             nc.sync.dma_start(tile_[:], src)
-        last_gate = keep.tile([P, V], F32, name="last_gate")
-        nc.sync.dma_start(out=last_gate[:], in_=gate[D - 1])
 
 
         gate_t = psum.tile([P, V], F32, name="gate_t", tag="bank4")
@@ -83,6 +81,18 @@ def tile_picked_grand_none_e_kernel(
             out=gate_sum[:], in_=gate_t[:, 0 : D * VT].rearrange("p (d t) -> p t d", d=D), axis=mybir.AxisListType.X, op=ADD
         )
         nc.vector.tensor_scalar(out=factor[:, 0:VT], in0=gate_sum[:], scalar1=-1.0, scalar2=1.0, op0=MULT, op1=ADD)
+
+        factor_rows = []
+        for d in range(D + 1):
+            spread = psum.tile([P, V], F32, name="spread", tag="bank%d" % d)
+            for t in range(VT):
+                col = d * VT + t
+                nc.tensor.transpose(
+                    spread[:, t * P : (t + 1) * P], factor[:, col : col + 1].to_broadcast([P, P]), ident[:]
+                )
+            row = keep.tile([P, V], F32, name="factor_row%d" % d)
+            nc.scalar.activation(out=row[:], in_=spread[:], func=COPY)
+            factor_rows.append(row)
 
         grouped = [keep.tile([P, HALF, PACK], BF16, name="grouped%d" % h, align_bytes=64) for h in range(2)]
         half_offs = [offs_sb[:, h * HALF // LIST : (h + 1) * HALF // LIST] for h in range(2)]
@@ -133,64 +143,57 @@ def tile_picked_grand_none_e_kernel(
         for h in (1, 0):
             product(1, h, slice(0, HALF), False, 2 + h)
 
-        turns = []
-
-        def turned_term(b, d, cols, total, first, final):
-            width = cols.stop - cols.start
-            tiles = width // P
-            picked = ring.tile([P, width], F32, name="picked", tag="picked")
-            nc.vector.tensor_copy(
-                out=picked[:], in_=y[b][:].indirect(lists[d][:, cols.start // LIST : cols.stop // LIST])
+        def weighted_term(b, d, cols, name):
+            term = ring.tile([P, cols.stop - cols.start], F32, name=name, tag=name)
+            nc.vector.tensor_tensor(
+                out=term[:],
+                in0=y[b][:].indirect(lists[d][:, cols.start // LIST : cols.stop // LIST]),
+                in1=factor_rows[d][:, cols],
+                op=MULT,
             )
-            turned = psum.tile([P, V], F32, name="turned", tag="bank%d" % ((4 + len(turns)) % 5))
-            turns.append(b)
+            return term
+
+        def add_turned(term, bank, first, final):
+            tiles = term.shape[1] // P
             for t in range(tiles):
-                nc.tensor.transpose(turned[:, t * P : (t + 1) * P], picked[:, t * P : (t + 1) * P], ident[:])
-            weighted = ring.tile([P, width], F32, name="weighted", tag="weighted")
-            for t in range(tiles):
-                col = d * VT + cols.start // P + t
-                nc.scalar.activation(
-                    out=weighted[:, t * P : (t + 1) * P],
-                    in_=turned[:, t * P : (t + 1) * P],
-                    func=COPY,
-                    scale=factor[:, col : col + 1],
-                )
-            for t in range(tiles):
-                vt = cols.start // P + t
-                bank, at = total(vt)
                 nc.tensor.matmul(
-                    bank[:, at * P : (at + 1) * P],
-                    lhsT=weighted[:, t * P : (t + 1) * P],
+                    bank[:, t * P : (t + 1) * P],
+                    lhsT=term[:, t * P : (t + 1) * P],
                     rhs=ident[:],
                     is_transpose=True,
-                    start=first and at == 0,
-                    stop=final(vt),
+                    start=first and t == 0,
+                    stop=final and t == tiles - 1,
                 )
+
+        def turn_back(bank, width, tag):
+            staged = keep.tile([P, width], F32, name="staged" + tag)
+            nc.scalar.activation(out=staged[:], in_=bank[:, 0:width], func=COPY)
+            back = psum.tile([P, V], F32, name="back", tag=tag)
+            for t in range(width // P):
+                nc.tensor.transpose(back[:, t * P : (t + 1) * P], staged[:, t * P : (t + 1) * P], ident[:])
+            return back
 
         whole = slice(0, V)
         total0 = psum.tile([P, V], F32, name="total0")
         for d in range(D + 1):
-            turned_term(0, d, whole, lambda vt: (total0, vt), d == 0, lambda vt: d == D and vt == VT - 1)
+            add_turned(weighted_term(0, d, whole, "term"), total0, d == 0, d == D)
+        back0 = turn_back(total0, V, "bank4")
         result0 = keep.tile([P, V], F32, name="result0")
-        nc.scalar.activation(out=result0[:], in_=total0[:], func=COPY)
+        nc.scalar.activation(out=result0[:], in_=back0[:], func=COPY)
         nc.sync.dma_start(out=out[0:P, :], in_=result0[:])
 
         total1 = [psum.tile([P, V], F32, name="total1_%d" % u) for u in range(2)]
-        for d in range(D):
-            pieces = [whole] if d < D - 1 else [slice(0, V // 2), slice(V // 2, V)]
-            for cols in pieces:
-                turned_term(
-                    1, d, cols, lambda vt: (total1[vt // 2], vt % 2), d == 0, lambda vt: d == D - 1 and vt % 2 == 1
-                )
+        halves = [slice(u * V // 2, (u + 1) * V // 2) for u in range(2)]
+        for d in range(D - 1):
+            term = weighted_term(1, d, whole, "term")
+            for u in range(2):
+                add_turned(term[:, halves[u]], total1[u], d == 0, False)
+        back1 = []
         for u in range(2):
-            cols = slice(u * V // 2, (u + 1) * V // 2)
-            pulled = keep.tile([P, V // 2], F32, name="pulled%d" % u)
-            nc.vector.tensor_tensor(
-                out=pulled[:],
-                in0=y[1][:].indirect(lists[D][:, cols.start // LIST : cols.stop // LIST]),
-                in1=last_gate[:, cols],
-                op=MULT,
-            )
+            add_turned(weighted_term(1, D - 1, halves[u], "term"), total1[u], False, True)
+            back1.append(turn_back(total1[u], V // 2, "bank%d" % u))
+        for u in range(2):
+            pulled = weighted_term(1, D, halves[u], "pulled")
             result1 = keep.tile([P, V // 2], F32, name="result1_%d" % u)
-            nc.vector.tensor_tensor(out=result1[:], in0=total1[u][:, 0 : V // 2], in1=pulled[:], op=ADD)
-            nc.sync.dma_start(out=out[P : 2 * P, cols], in_=result1[:])
+            nc.vector.tensor_tensor(out=result1[:], in0=back1[u][:, 0 : V // 2], in1=pulled[:], op=ADD)
+            nc.sync.dma_start(out=out[P : 2 * P, halves[u]], in_=result1[:])

@@ -21,10 +21,10 @@ ADD = mybir.AluOpType.add
 P = 128
 PACK = 4
 HALF = S // 2
-QUARTER = S // 4
 LIST = 16
 VT = V // P
-LAST_PLANE_CHUNKS = (1024, 1024, 1024, 768, 256)
+LAST_PLANE_LOADS = ((1280, 0), (1024, 0), (1024, 1024), (512, 384), (256, 0))
+PIECES = ((1, 0, 256, False), (1, 256, 256, False), (0, 0, 256, True), (0, 256, 128, False), (0, 384, 128, True))
 
 
 def tile_picked_grand_none_e_kernel(
@@ -35,6 +35,9 @@ def tile_picked_grand_none_e_kernel(
         keep = ctx.enter_context(tc.tile_pool(name="keep", bufs=1))
         ring = ctx.enter_context(tc.tile_pool(name="ring", bufs=4))
         psum = ctx.enter_context(tc.psum_pool(name="psum", bufs=1))
+
+        def bank(number):
+            return psum.tile([P, V], F32, name="bank", tag="bank%d" % number)
 
         offs_sb = keep.tile([P, S // LIST], U16, name="offs_sb")
         lists = [keep.tile([P, V // LIST], U16, name="list%d" % i) for i in range(D + 1)]
@@ -55,13 +58,11 @@ def tile_picked_grand_none_e_kernel(
         nc.sync.dma_start(out=gate_rows[0 : D * VT, :], in_=gate_flat[0 : (D * VT - 1) * stride + 1 : stride, :])
         for j in range(1, PACK - 1):
             nc.sync.dma_start(out=planes[j][:], in_=rows[:, j, :])
-        chunks = []
+        last_plane = planes[PACK - 1]
         c0 = 0
-        for width in LAST_PLANE_CHUNKS:
-            chunks.append(slice(c0, c0 + width))
+        for width, on_vector in LAST_PLANE_LOADS:
+            nc.sync.dma_start(out=last_plane[:, c0 : c0 + width], in_=rows[:, PACK - 1, c0 : c0 + width])
             c0 = c0 + width
-        for cols in chunks:
-            nc.sync.dma_start(out=planes[PACK - 1][:, cols], in_=rows[:, PACK - 1, cols])
         w_codes = keep.tile([P, 2 * N], U8, name="w_codes", align_bytes=64)
         nc.sync.dma_start(out=w_codes[:], in_=w1_words[0])
         for q in range(4):
@@ -71,8 +72,7 @@ def tile_picked_grand_none_e_kernel(
         for tile_, src in zip(lists, (cen, pos1, pos2, pos3)):
             nc.sync.dma_start(tile_[:], src)
 
-
-        gate_t = psum.tile([P, V], F32, name="gate_t", tag="bank4")
+        gate_t = bank(4)
         nc.tensor.transpose(gate_t[:, 0:P], gate_rows[:], ident[:])
         factor = keep.tile([P, (D + 1) * VT], F32, name="factor")
         gate_sum = keep.tile([P, VT], F32, name="gate_sum")
@@ -84,7 +84,7 @@ def tile_picked_grand_none_e_kernel(
 
         factor_rows = []
         for d in range(D + 1):
-            spread = psum.tile([P, V], F32, name="spread", tag="bank%d" % d)
+            spread = bank(d)
             for t in range(VT):
                 col = d * VT + t
                 nc.tensor.transpose(
@@ -100,20 +100,23 @@ def tile_picked_grand_none_e_kernel(
             for h in range(2):
                 nc.vector.tensor_copy(out=grouped[h][:, :, j], in_=planes[j][:].indirect(half_offs[h]))
         last_bf = keep.tile([P, T], BF16, name="last_bf")
-        for i, cols in enumerate(chunks):
-            if i == 3:
-                nc.vector.tensor_copy(out=last_bf[:, cols], in_=planes[PACK - 1][:, cols])
-            else:
-                nc.scalar.activation(out=last_bf[:, cols], in_=planes[PACK - 1][:, cols], func=COPY)
-        nc.vector.tensor_copy(out=grouped[1][:, :, PACK - 1], in_=planes[PACK - 1][:].indirect(half_offs[1]))
+        c0 = 0
+        for width, on_vector in LAST_PLANE_LOADS:
+            split = c0 + on_vector
+            if on_vector > 0:
+                nc.vector.tensor_copy(out=last_bf[:, c0:split], in_=last_plane[:, c0:split])
+            if on_vector < width:
+                nc.scalar.activation(out=last_bf[:, split : c0 + width], in_=last_plane[:, split : c0 + width], func=COPY)
+            c0 = c0 + width
+        nc.vector.tensor_copy(out=grouped[1][:, :, PACK - 1], in_=last_plane[:].indirect(half_offs[1]))
         nc.scalar.activation(out=grouped[0][:, :, PACK - 1], in_=last_bf[:].indirect(half_offs[0]), func=COPY)
 
         codes = [keep.tile([P, HALF], U32, name="codes%d" % h, align_bytes=64) for h in range(2)]
         scales = [keep.tile([P, HALF], U8, name="scales%d" % h, align_bytes=64) for h in range(2)]
         y = [keep.tile([P, S], F32, name="y%d" % b) for b in range(2)]
 
-        def product(b, h, cols, last, bank):
-            acc = psum.tile([P, V], F32, name="acc", tag="bank%d" % bank)
+        def product(b, h, cols, on_vector, number):
+            acc = bank(number)
             width = cols.stop - cols.start
             nc.tensor.matmul_mx(
                 out=acc[:, 0:width],
@@ -125,23 +128,22 @@ def tile_picked_grand_none_e_kernel(
                 stop=True,
             )
             dst = y[b][:, h * HALF + cols.start : h * HALF + cols.stop]
-            if last:
+            if on_vector:
                 nc.vector.tensor_copy(out=dst, in_=acc[:, 0:width])
             else:
                 nc.scalar.activation(out=dst, in_=acc[:, 0:width], func=COPY)
 
-        for h in (1, 0):
+        for i, (h, first, count, on_vector) in enumerate(PIECES):
+            cols = slice(first, first + count)
             flat = grouped[h][:].rearrange("p n j -> p (n j)")
-            for u in range(2):
-                cols = slice(u * QUARTER, (u + 1) * QUARTER)
-                nc.vector.quantize_mx(
-                    out=codes[h][:, cols].bitcast(FP8X4),
-                    scales=scales[h][:, cols],
-                    in_=flat[:, PACK * cols.start : PACK * cols.stop],
-                )
-                product(0, h, cols, h == 0 and u == 1, 2 * (1 - h) + u)
+            nc.vector.quantize_mx(
+                out=codes[h][:, cols].bitcast(FP8X4),
+                scales=scales[h][:, cols],
+                in_=flat[:, PACK * cols.start : PACK * cols.stop],
+            )
+            product(0, h, cols, on_vector, i)
         for h in (1, 0):
-            product(1, h, slice(0, HALF), False, 2 + h)
+            product(1, h, slice(0, HALF), False, len(PIECES) - 1 - h)
 
         def weighted_term(b, d, cols, name):
             term = ring.tile([P, cols.stop - cols.start], F32, name=name, tag=name)
@@ -153,11 +155,11 @@ def tile_picked_grand_none_e_kernel(
             )
             return term
 
-        def add_turned(term, bank, first, final):
+        def add_turned(term, total, first, final):
             tiles = term.shape[1] // P
             for t in range(tiles):
                 nc.tensor.matmul(
-                    bank[:, t * P : (t + 1) * P],
+                    total[:, t * P : (t + 1) * P],
                     lhsT=term[:, t * P : (t + 1) * P],
                     rhs=ident[:],
                     is_transpose=True,
@@ -165,35 +167,45 @@ def tile_picked_grand_none_e_kernel(
                     stop=final and t == tiles - 1,
                 )
 
-        def turn_back(bank, width, tag):
-            staged = keep.tile([P, width], F32, name="staged" + tag)
-            nc.scalar.activation(out=staged[:], in_=bank[:, 0:width], func=COPY)
-            back = psum.tile([P, V], F32, name="back", tag=tag)
+        def turn_back(total, back, name):
+            width = total.shape[1]
+            staged = keep.tile([P, width], F32, name=name)
+            nc.scalar.activation(out=staged[:], in_=total, func=COPY)
             for t in range(width // P):
                 nc.tensor.transpose(back[:, t * P : (t + 1) * P], staged[:, t * P : (t + 1) * P], ident[:])
-            return back
 
         whole = slice(0, V)
-        total0 = psum.tile([P, V], F32, name="total0")
+        total0 = bank(5)
         for d in range(D + 1):
-            add_turned(weighted_term(0, d, whole, "term"), total0, d == 0, d == D)
-        back0 = turn_back(total0, V, "bank4")
+            add_turned(weighted_term(0, d, whole, "term"), total0[:], d == 0, d == D)
+        back0 = bank(6)
+        turn_back(total0[:], back0[:], "staged0")
         result0 = keep.tile([P, V], F32, name="result0")
         nc.scalar.activation(out=result0[:], in_=back0[:], func=COPY)
         nc.sync.dma_start(out=out[0:P, :], in_=result0[:])
 
-        total1 = [psum.tile([P, V], F32, name="total1_%d" % u) for u in range(2)]
-        halves = [slice(u * V // 2, (u + 1) * V // 2) for u in range(2)]
+        quarters = [slice(t * P, (t + 1) * P) for t in range(VT)]
+        sums = [bank(number) for number in (0, 1, 2, 7)]
         for d in range(D - 1):
             term = weighted_term(1, d, whole, "term")
-            for u in range(2):
-                add_turned(term[:, halves[u]], total1[u], d == 0, False)
-        back1 = []
-        for u in range(2):
-            add_turned(weighted_term(1, D - 1, halves[u], "term"), total1[u], False, True)
-            back1.append(turn_back(total1[u], V // 2, "bank%d" % u))
-        for u in range(2):
-            pulled = weighted_term(1, D, halves[u], "pulled")
-            result1 = keep.tile([P, V // 2], F32, name="result1_%d" % u)
-            nc.vector.tensor_tensor(out=result1[:], in0=back1[u][:, 0 : V // 2], in1=pulled[:], op=ADD)
-            nc.sync.dma_start(out=out[P : 2 * P, halves[u]], in_=result1[:])
+            for t in range(VT):
+                add_turned(term[:, quarters[t]], sums[t][:, 0:P], d == 0, False)
+        for t in range(VT):
+            add_turned(weighted_term(1, D - 1, quarters[t], "part"), sums[t][:, 0:P], False, True)
+            turn_back(sums[t][:, 0:P], sums[t][:, P : 2 * P], "staged1_%d" % t)
+        last_term = keep.tile([P, V], F32, name="last_term")
+        for cols in (slice(0, 3 * P), slice(3 * P, V)):
+            nc.vector.tensor_tensor(
+                out=last_term[:, cols],
+                in0=y[1][:].indirect(lists[D][:, cols.start // LIST : cols.stop // LIST]),
+                in1=factor_rows[D][:, cols],
+                op=MULT,
+            )
+        result1 = keep.tile([P, V], F32, name="result1")
+        for t in range(VT):
+            nc.vector.tensor_tensor(
+                out=result1[:, quarters[t]], in0=sums[t][:, P : 2 * P], in1=last_term[:, quarters[t]], op=ADD
+            )
+            if t > 0:
+                cols = slice(0 if t == 1 else t * P, (t + 1) * P)
+                nc.sync.dma_start(out=out[P : 2 * P, cols], in_=result1[:, cols])

@@ -23,7 +23,7 @@ PACK = 4
 HALF = S // 2
 LIST = 16
 VT = V // P
-LAST_PLANE_LOADS = ((1280, 0), (1024, 0), (1024, 1024), (512, 384), (256, 0))
+LAST_PLANE_LOADS = ((1024, 0), (1024, 0), (1024, 0), (768, 768), (256, 0))
 PIECES = ((1, 0, 256, False), (1, 256, 256, False), (0, 0, 256, True), (0, 256, 128, False), (0, 384, 128, True))
 
 

@@ -175,11 +175,23 @@ def tile_picked_grand_none_e_kernel(
                 nc.tensor.transpose(back[:, t * P : (t + 1) * P], staged[:, t * P : (t + 1) * P], ident[:])
 
         whole = slice(0, V)
-        total0 = bank(5)
-        for d in range(D + 1):
-            add_turned(weighted_term(0, d, whole, "term"), total0[:], d == 0, d == D)
         back0 = bank(6)
-        turn_back(total0[:], back0[:], "staged0")
+        for d in range(D + 1):
+            plain = keep.tile([P, V], F32, name="plain%d" % d)
+            nc.vector.tensor_copy(out=plain[:], in_=y[0][:].indirect(lists[d][:]))
+            turned = bank(5 if d % 2 == 0 else 7)
+            for t in range(VT):
+                nc.tensor.transpose(turned[:, t * P : (t + 1) * P], plain[:, t * P : (t + 1) * P], ident[:])
+            scaled = keep.tile([P, V], F32, name="scaled%d" % d)
+            for t in range(VT):
+                col = d * VT + t
+                nc.scalar.activation(
+                    out=scaled[:, t * P : (t + 1) * P],
+                    in_=turned[:, t * P : (t + 1) * P],
+                    func=COPY,
+                    scale=factor[:, col : col + 1],
+                )
+            add_turned(scaled[:], back0[:], d == 0, d == D)
         result0 = keep.tile([P, V], F32, name="result0")
         nc.scalar.activation(out=result0[:], in_=back0[:], func=COPY)
         nc.sync.dma_start(out=out[0:P, :], in_=result0[:])

@@ -25,6 +25,9 @@ LIST = 16
 VT = V // P
 LAST_PLANE_LOADS = ((1024, 0), (1024, 0), (1024, 0), (768, 768), (256, 0))
 PIECES = ((1, 0, 256, False), (1, 256, 256, False), (0, 0, 256, True), (0, 256, 128, False), (0, 384, 128, True))
+TURN_BANKS = ((0, 1, 2, 5), (3, 4, 7, 7), (0, 1, 2, 5), (3, 4, 7, 7))
+Y1_BANKS = (4, 3)
+SUM_BANKS = (0, 1, 2, 7)
 
 
 def tile_picked_grand_none_e_kernel(
@@ -143,7 +146,7 @@ def tile_picked_grand_none_e_kernel(
             )
             product(0, h, cols, on_vector, i)
         for h in (1, 0):
-            product(1, h, slice(0, HALF), False, len(PIECES) - 1 - h)
+            product(1, h, slice(0, HALF), False, Y1_BANKS[h])
 
         def weighted_term(b, d, cols, name):
             term = ring.tile([P, cols.stop - cols.start], F32, name=name, tag=name)
@@ -179,17 +182,15 @@ def tile_picked_grand_none_e_kernel(
         for d in range(D + 1):
             plain = keep.tile([P, V], F32, name="plain%d" % d)
             nc.vector.tensor_copy(out=plain[:], in_=y[0][:].indirect(lists[d][:]))
-            turned = bank(5 if d % 2 == 0 else 7)
+            banks = {number: bank(number) for number in sorted(set(TURN_BANKS[d]))}
+            turned = [banks[TURN_BANKS[d][t]][:, t * P : (t + 1) * P] for t in range(VT)]
             for t in range(VT):
-                nc.tensor.transpose(turned[:, t * P : (t + 1) * P], plain[:, t * P : (t + 1) * P], ident[:])
+                nc.tensor.transpose(turned[t], plain[:, t * P : (t + 1) * P], ident[:])
             scaled = keep.tile([P, V], F32, name="scaled%d" % d)
             for t in range(VT):
                 col = d * VT + t
                 nc.scalar.activation(
-                    out=scaled[:, t * P : (t + 1) * P],
-                    in_=turned[:, t * P : (t + 1) * P],
-                    func=COPY,
-                    scale=factor[:, col : col + 1],
+                    out=scaled[:, t * P : (t + 1) * P], in_=turned[t], func=COPY, scale=factor[:, col : col + 1]
                 )
             add_turned(scaled[:], back0[:], d == 0, d == D)
         result0 = keep.tile([P, V], F32, name="result0")
@@ -197,7 +198,7 @@ def tile_picked_grand_none_e_kernel(
         nc.sync.dma_start(out=out[0:P, :], in_=result0[:])
 
         quarters = [slice(t * P, (t + 1) * P) for t in range(VT)]
-        sums = [bank(number) for number in (0, 1, 2, 7)]
+        sums = [bank(number) for number in SUM_BANKS]
         for d in range(D - 1):
             term = weighted_term(1, d, whole, "term")
             for t in range(VT):

@@ -23,7 +23,7 @@ PACK = 4
 HALF = S // 2
 LIST = 16
 VT = V // P
-LAST_PLANE_LOADS = ((1024, 0), (1024, 0), (1024, 0), (768, 768), (256, 0))
+LAST_PLANE_LOADS = ((1280, 0), (1024, 0), (1024, 1024), (512, 384), (256, 0))
 PIECES = ((1, 0, 256, False), (1, 256, 256, False), (0, 0, 256, True), (0, 256, 128, False), (0, 384, 128, True))
 TURN_BANKS = ((0, 1, 2, 5), (3, 4, 7, 7), (0, 1, 2, 5), (3, 4, 7, 7))
 Y1_BANKS = (4, 3)
@@ -203,9 +203,11 @@ def tile_picked_grand_none_e_kernel(
             term = weighted_term(1, d, whole, "term")
             for t in range(VT):
                 add_turned(term[:, quarters[t]], sums[t][:, 0:P], d == 0, False)
-        for t in range(VT):
-            add_turned(weighted_term(1, D - 1, quarters[t], "part"), sums[t][:, 0:P], False, True)
-            turn_back(sums[t][:, 0:P], sums[t][:, P : 2 * P], "staged1_%d" % t)
+        for group in ((0, 1), (2,), (3,)):
+            part = weighted_term(1, D - 1, slice(group[0] * P, (group[-1] + 1) * P), "part")
+            for t in group:
+                add_turned(part[:, (t - group[0]) * P : (t - group[0] + 1) * P], sums[t][:, 0:P], False, True)
+                turn_back(sums[t][:, 0:P], sums[t][:, P : 2 * P], "staged1_%d" % t)
         last_term = keep.tile([P, V], F32, name="last_term")
         for cols in (slice(0, 3 * P), slice(3 * P, V)):
             nc.vector.tensor_tensor(

@@ -23,7 +23,7 @@ PACK = 4
 HALF = S // 2
 LIST = 16
 VT = V // P
-LAST_PLANE_LOADS = ((1280, 0), (1024, 0), (1024, 1024), (512, 384), (256, 0))
+LAST_PLANE_LOADS = ((1280, 0), (1152, 0), (896, 896), (512, 320), (256, 0))
 PIECES = ((1, 0, 256, False), (1, 256, 256, False), (0, 0, 256, True), (0, 256, 128, False), (0, 384, 128, True))
 TURN_BANKS = ((0, 1, 2, 5), (3, 4, 7, 7), (0, 1, 2, 5), (3, 4, 7, 7))
 Y1_BANKS = (4, 3)

@@ -24,7 +24,7 @@ HALF = S // 2
 LIST = 16
 VT = V // P
 LAST_PLANE_LOADS = ((1280, 0), (1152, 0), (896, 896), (512, 320), (256, 0))
-PIECES = ((1, 0, 256, False), (1, 256, 256, False), (0, 0, 256, True), (0, 256, 128, False), (0, 384, 128, True))
+PIECES = ((1, 0, 256, False), (1, 256, 256, False), (0, 0, 256, True), (0, 256, 128, False), (0, 384, 128, False))
 TURN_BANKS = ((0, 1, 2, 5), (3, 4, 7, 7), (0, 1, 2, 5), (3, 4, 7, 7))
 Y1_BANKS = (4, 3)
 SUM_BANKS = (0, 1, 2, 7)

@@ -25,9 +25,8 @@ LIST = 16
 VT = V // P
 LAST_PLANE_LOADS = ((1280, 0), (1152, 0), (896, 896), (512, 320), (256, 0))
 PIECES = ((1, 0, 256, False), (1, 256, 256, False), (0, 0, 256, True), (0, 256, 128, False), (0, 384, 128, False))
-TURN_BANKS = ((0, 1, 2, 5), (3, 4, 7, 7), (0, 1, 2, 5), (3, 4, 7, 7))
 Y1_BANKS = (4, 3)
-SUM_BANKS = (0, 1, 2, 7)
+SPAN = V // 2
 
 
 def tile_picked_grand_none_e_kernel(
@@ -36,7 +35,6 @@ def tile_picked_grand_none_e_kernel(
     nc = tc.nc
     with ExitStack() as ctx:
         keep = ctx.enter_context(tc.tile_pool(name="keep", bufs=1))
-        ring = ctx.enter_context(tc.tile_pool(name="ring", bufs=4))
         psum = ctx.enter_context(tc.psum_pool(name="psum", bufs=1))
 
         def bank(number):
@@ -148,79 +146,89 @@ def tile_picked_grand_none_e_kernel(
         for h in (1, 0):
             product(1, h, slice(0, HALF), False, Y1_BANKS[h])
 
-        def weighted_term(b, d, cols, name):
-            term = ring.tile([P, cols.stop - cols.start], F32, name=name, tag=name)
-            nc.vector.tensor_tensor(
-                out=term[:],
-                in0=y[b][:].indirect(lists[d][:, cols.start // LIST : cols.stop // LIST]),
-                in1=factor_rows[d][:, cols],
-                op=MULT,
-            )
-            return term
+        sums = {(b, s): bank(2 * b + s) for b in range(2) for s in range(2)}
+        added = {unit: 0 for unit in sums}
+        terms = {(b, d): keep.tile([P, V], F32, name="term%d%d" % (b, d)) for b in range(2) for d in range(D + 1)}
+        plains = {}
+        result = [keep.tile([P, V], F32, name="result%d" % b) for b in range(2)]
+        both, low, high = (0, 1), (0,), (1,)
 
-        def add_turned(term, total, first, final):
-            tiles = term.shape[1] // P
-            for t in range(tiles):
-                nc.tensor.matmul(
-                    total[:, t * P : (t + 1) * P],
-                    lhsT=term[:, t * P : (t + 1) * P],
-                    rhs=ident[:],
-                    is_transpose=True,
-                    start=first and t == 0,
-                    stop=final and t == tiles - 1,
+        def span(halves):
+            return slice(halves[0] * SPAN, (halves[-1] + 1) * SPAN)
+
+        def lookup(b, d, halves):
+            cols = span(halves)
+            return y[b][:].indirect(lists[d][:, cols.start // LIST : cols.stop // LIST])
+
+        def add_turned(b, d, halves):
+            if d == D:
+                return
+            for s in halves:
+                for t in range(SPAN // P):
+                    first = s * SPAN + t * P
+                    nc.tensor.matmul(
+                        sums[b, s][:, t * P : (t + 1) * P],
+                        lhsT=terms[b, d][:, first : first + P],
+                        rhs=ident[:],
+                        is_transpose=True,
+                        start=added[b, s] == 0 and t == 0,
+                        stop=added[b, s] == D - 1 and t == SPAN // P - 1,
+                    )
+                added[b, s] = added[b, s] + 1
+
+        def fused(b, d, halves):
+            cols = span(halves)
+            nc.vector.tensor_tensor(
+                out=terms[b, d][:, cols], in0=lookup(b, d, halves), in1=factor_rows[d][:, cols], op=MULT
+            )
+            add_turned(b, d, halves)
+
+        def fetch(b, d, halves):
+            if (b, d) not in plains:
+                plains[b, d] = keep.tile([P, V], F32, name="plain%d%d" % (b, d))
+            nc.scalar.activation(out=plains[b, d][:, span(halves)], in_=lookup(b, d, halves), func=COPY)
+
+        def weigh(b, d, halves):
+            cols = span(halves)
+            nc.vector.tensor_tensor(
+                out=terms[b, d][:, cols], in0=plains[b, d][:, cols], in1=factor_rows[d][:, cols], op=MULT
+            )
+            add_turned(b, d, halves)
+
+        def turn_back(b, s):
+            staged = keep.tile([P, SPAN], F32, name="staged%d%d" % (b, s))
+            nc.scalar.activation(out=staged[:], in_=sums[b, s][:, 0:SPAN], func=COPY)
+            for t in range(SPAN // P):
+                nc.tensor.transpose(
+                    sums[b, s][:, SPAN + t * P : SPAN + (t + 1) * P], staged[:, t * P : (t + 1) * P], ident[:]
                 )
 
-        def turn_back(total, back, name):
-            width = total.shape[1]
-            staged = keep.tile([P, width], F32, name=name)
-            nc.scalar.activation(out=staged[:], in_=total, func=COPY)
-            for t in range(width // P):
-                nc.tensor.transpose(back[:, t * P : (t + 1) * P], staged[:, t * P : (t + 1) * P], ident[:])
-
-        whole = slice(0, V)
-        back0 = bank(6)
-        for d in range(D + 1):
-            plain = keep.tile([P, V], F32, name="plain%d" % d)
-            nc.vector.tensor_copy(out=plain[:], in_=y[0][:].indirect(lists[d][:]))
-            banks = {number: bank(number) for number in sorted(set(TURN_BANKS[d]))}
-            turned = [banks[TURN_BANKS[d][t]][:, t * P : (t + 1) * P] for t in range(VT)]
-            for t in range(VT):
-                nc.tensor.transpose(turned[t], plain[:, t * P : (t + 1) * P], ident[:])
-            scaled = keep.tile([P, V], F32, name="scaled%d" % d)
-            for t in range(VT):
-                col = d * VT + t
-                nc.scalar.activation(
-                    out=scaled[:, t * P : (t + 1) * P], in_=turned[t], func=COPY, scale=factor[:, col : col + 1]
-                )
-            add_turned(scaled[:], back0[:], d == 0, d == D)
-        result0 = keep.tile([P, V], F32, name="result0")
-        nc.scalar.activation(out=result0[:], in_=back0[:], func=COPY)
-        nc.sync.dma_start(out=out[0:P, :], in_=result0[:])
-
-        quarters = [slice(t * P, (t + 1) * P) for t in range(VT)]
-        sums = [bank(number) for number in SUM_BANKS]
-        for d in range(D - 1):
-            term = weighted_term(1, d, whole, "term")
-            for t in range(VT):
-                add_turned(term[:, quarters[t]], sums[t][:, 0:P], d == 0, False)
-        for group in ((0, 1), (2,), (3,)):
-            part = weighted_term(1, D - 1, slice(group[0] * P, (group[-1] + 1) * P), "part")
-            for t in group:
-                add_turned(part[:, (t - group[0]) * P : (t - group[0] + 1) * P], sums[t][:, 0:P], False, True)
-                turn_back(sums[t][:, 0:P], sums[t][:, P : 2 * P], "staged1_%d" % t)
-        last_term = keep.tile([P, V], F32, name="last_term")
-        for cols in (slice(0, 3 * P), slice(3 * P, V)):
+        def finish(b, s):
+            cols = span((s,))
             nc.vector.tensor_tensor(
-                out=last_term[:, cols],
-                in0=y[1][:].indirect(lists[D][:, cols.start // LIST : cols.stop // LIST]),
-                in1=factor_rows[D][:, cols],
-                op=MULT,
+                out=result[b][:, cols], in0=sums[b, s][:, SPAN : 2 * SPAN], in1=terms[b, D][:, cols], op=ADD
             )
-        result1 = keep.tile([P, V], F32, name="result1")
-        for t in range(VT):
-            nc.vector.tensor_tensor(
-                out=result1[:, quarters[t]], in0=sums[t][:, P : 2 * P], in1=last_term[:, quarters[t]], op=ADD
-            )
-            if t > 0:
-                cols = slice(0 if t == 1 else t * P, (t + 1) * P)
-                nc.sync.dma_start(out=out[P : 2 * P, cols], in_=result1[:, cols])
+            nc.sync.dma_start(out=out[b * P : (b + 1) * P, cols], in_=result[b][:, cols])
+
+        fused(0, 0, both)
+        fetch(0, 1, both)
+        fused(1, 0, both)
+        fetch(0, 2, both)
+        weigh(0, 1, both)
+        fused(1, 1, both)
+        fetch(1, 2, both)
+        weigh(0, 2, both)
+        fetch(0, 3, both)
+        weigh(1, 2, both)
+        turn_back(0, 0)
+        turn_back(0, 1)
+        fused(1, 3, low)
+        turn_back(1, 0)
+        turn_back(1, 1)
+        fetch(1, 3, high)
+        weigh(0, 3, both)
+        finish(0, 0)
+        finish(0, 1)
+        weigh(1, 3, high)
+        finish(1, 0)
+        finish(1, 1)

@@ -183,7 +183,9 @@ def tile_picked_grand_none_e_kernel(
             )
             add_turned(b, d, halves)
 
-        def fetch(b, d, halves):
+        def fetch(b, d, halves, into=None):
+            if into is not None:
+                plains[b, d] = terms[into]
             if (b, d) not in plains:
                 plains[b, d] = keep.tile([P, V], F32, name="plain%d%d" % (b, d))
             nc.scalar.activation(out=plains[b, d][:, span(halves)], in_=lookup(b, d, halves), func=COPY)
@@ -212,23 +214,22 @@ def tile_picked_grand_none_e_kernel(
 
         fused(0, 0, both)
         fetch(0, 1, both)
-        fused(1, 0, both)
-        fetch(0, 2, both)
         weigh(0, 1, both)
-        fused(1, 1, both)
+        fused(0, 2, both)
+        fetch(1, 1, both)
+        fused(1, 0, both)
         fetch(1, 2, both)
-        weigh(0, 2, both)
-        fetch(0, 3, both)
+        weigh(1, 1, both)
         weigh(1, 2, both)
         turn_back(0, 0)
         turn_back(0, 1)
-        fused(1, 3, low)
+        fetch(1, 3, both, into=(0, 2))
+        terms[0, 3] = plains[1, 2]
+        fused(0, 3, both)
         turn_back(1, 0)
         turn_back(1, 1)
-        fetch(1, 3, high)
-        weigh(0, 3, both)
+        weigh(1, 3, both)
         finish(0, 0)
         finish(0, 1)
-        weigh(1, 3, high)
         finish(1, 0)
         finish(1, 1)

@@ -25,7 +25,7 @@ LIST = 16
 VT = V // P
 LAST_PLANE_LOADS = ((1280, 0), (1152, 0), (896, 896), (512, 320), (256, 0))
 PIECES = ((1, 0, 256, False), (1, 256, 256, False), (0, 0, 256, True), (0, 256, 128, False), (0, 384, 128, False))
-Y1_BANKS = (4, 3)
+Y1_BANKS = (3, 2)
 SPAN = V // 2
 
 
@@ -83,17 +83,19 @@ def tile_picked_grand_none_e_kernel(
         )
         nc.vector.tensor_scalar(out=factor[:, 0:VT], in0=gate_sum[:], scalar1=-1.0, scalar2=1.0, op0=MULT, op1=ADD)
 
-        factor_rows = []
+        factor_rows = {}
+        factor_banks = {}
         for d in range(D + 1):
-            spread = bank(d)
+            spread = bank((0, 1, 2, 3)[d])
+            factor_banks[d] = spread
             for t in range(VT):
                 col = d * VT + t
                 nc.tensor.transpose(
                     spread[:, t * P : (t + 1) * P], factor[:, col : col + 1].to_broadcast([P, P]), ident[:]
                 )
-            row = keep.tile([P, V], F32, name="factor_row%d" % d)
-            nc.scalar.activation(out=row[:], in_=spread[:], func=COPY)
-            factor_rows.append(row)
+            if d in (0, 1, 2, 3,):
+                factor_rows[d] = keep.tile([P, V], F32, name="factor_row%d" % d)
+                nc.scalar.activation(out=factor_rows[d][:], in_=spread[:], func=COPY)
 
         grouped = [keep.tile([P, HALF, PACK], BF16, name="grouped%d" % h, align_bytes=64) for h in range(2)]
         half_offs = [offs_sb[:, h * HALF // LIST : (h + 1) * HALF // LIST] for h in range(2)]
@@ -183,12 +185,29 @@ def tile_picked_grand_none_e_kernel(
             )
             add_turned(b, d, halves)
 
-        def fetch(b, d, halves, into=None):
-            if into is not None:
-                plains[b, d] = terms[into]
+        def fetch(b, d, halves):
             if (b, d) not in plains:
                 plains[b, d] = keep.tile([P, V], F32, name="plain%d%d" % (b, d))
             nc.scalar.activation(out=plains[b, d][:, span(halves)], in_=lookup(b, d, halves), func=COPY)
+
+        def fetch_on_vector(b, d, halves):
+            if (b, d) not in plains:
+                plains[b, d] = keep.tile([P, V], F32, name="plain%d%d" % (b, d))
+            nc.vector.tensor_copy(out=plains[b, d][:, span(halves)], in_=lookup(b, d, halves))
+
+        def weigh_on_gpsimd(b, d, halves):
+            cols = span(halves)
+            nc.gpsimd.tensor_tensor(
+                out=terms[b, d][:, cols], in0=plains[b, d][:, cols], in1=factor_rows[d][:, cols], op=MULT
+            )
+            add_turned(b, d, halves)
+
+        def weigh_from_bank(b, d, halves):
+            cols = span(halves)
+            nc.vector.tensor_tensor(
+                out=terms[b, d][:, cols], in0=plains[b, d][:, cols], in1=factor_banks[d][:, cols], op=MULT
+            )
+            add_turned(b, d, halves)
 
         def weigh(b, d, halves):
             cols = span(halves)
@@ -214,22 +233,22 @@ def tile_picked_grand_none_e_kernel(
 
         fused(0, 0, both)
         fetch(0, 1, both)
-        weigh(0, 1, both)
         fused(0, 2, both)
-        fetch(1, 1, both)
-        fused(1, 0, both)
-        fetch(1, 2, both)
-        weigh(1, 1, both)
-        weigh(1, 2, both)
+        weigh(0, 1, both)
+        fetch(0, 3, both)
         turn_back(0, 0)
         turn_back(0, 1)
-        fetch(1, 3, both, into=(0, 2))
-        terms[0, 3] = plains[1, 2]
-        fused(0, 3, both)
+        fused(1, 0, both)
+        fetch(1, 1, both)
+        fused(1, 2, both)
+        weigh(1, 1, both)
+        terms[0, 3] = plains[1, 1]
+        weigh(0, 3, both)
+        fetch(1, 3, both)
+        finish(0, 0)
+        finish(0, 1)
         turn_back(1, 0)
         turn_back(1, 1)
         weigh(1, 3, both)
-        finish(0, 0)
-        finish(0, 1)
         finish(1, 0)
         finish(1, 1)

@@ -224,6 +224,16 @@ def tile_picked_grand_none_e_kernel(
                     sums[b, s][:, SPAN + t * P : SPAN + (t + 1) * P], staged[:, t * P : (t + 1) * P], ident[:]
                 )
 
+        def finish_tile(b, s, t):
+            cols = slice(s * SPAN + t * P, s * SPAN + (t + 1) * P)
+            nc.vector.tensor_tensor(
+                out=result[b][:, cols],
+                in0=sums[b, s][:, SPAN + t * P : SPAN + (t + 1) * P],
+                in1=terms[b, D][:, cols],
+                op=ADD,
+            )
+            nc.sync.dma_start(out=out[b * P : (b + 1) * P, cols], in_=result[b][:, cols])
+
         def finish(b, s):
             cols = span((s,))
             nc.vector.tensor_tensor(
@@ -236,10 +246,10 @@ def tile_picked_grand_none_e_kernel(
         fused(0, 2, both)
         weigh(0, 1, both)
         fetch(0, 3, both)
-        turn_back(0, 0)
-        turn_back(0, 1)
         fused(1, 0, both)
         fetch(1, 1, both)
+        turn_back(0, 0)
+        turn_back(0, 1)
         fused(1, 2, both)
         weigh(1, 1, both)
         terms[0, 3] = plains[1, 1]
@@ -251,4 +261,5 @@ def tile_picked_grand_none_e_kernel(
         turn_back(1, 1)
         weigh(1, 3, both)
         finish(1, 0)
-        finish(1, 1)
+        for t in range(SPAN // P):
+            finish_tile(1, 1, t)

@@ -25,7 +25,7 @@ LIST = 16
 VT = V // P
 LAST_PLANE_LOADS = ((1280, 0), (1152, 0), (896, 896), (512, 320), (256, 0))
 PIECES = ((1, 0, 256, False), (1, 256, 256, False), (0, 0, 256, True), (0, 256, 128, False), (0, 384, 128, False))
-Y1_BANKS = (3, 2)
+Y1_PIECES = ((1, 0, 256, 5), (1, 256, 256, 3), (0, 0, 512, 4))
 SPAN = V // 2
 
 
@@ -145,8 +145,8 @@ def tile_picked_grand_none_e_kernel(
                 in_=flat[:, PACK * cols.start : PACK * cols.stop],
             )
             product(0, h, cols, on_vector, i)
-        for h in (1, 0):
-            product(1, h, slice(0, HALF), False, Y1_BANKS[h])
+        for h, first, count, number in Y1_PIECES:
+            product(1, h, slice(first, first + count), False, number)
 
         sums = {(b, s): bank(2 * b + s) for b in range(2) for s in range(2)}
         added = {unit: 0 for unit in sums}
@@ -224,16 +224,6 @@ def tile_picked_grand_none_e_kernel(
                     sums[b, s][:, SPAN + t * P : SPAN + (t + 1) * P], staged[:, t * P : (t + 1) * P], ident[:]
                 )
 
-        def finish_tile(b, s, t):
-            cols = slice(s * SPAN + t * P, s * SPAN + (t + 1) * P)
-            nc.vector.tensor_tensor(
-                out=result[b][:, cols],
-                in0=sums[b, s][:, SPAN + t * P : SPAN + (t + 1) * P],
-                in1=terms[b, D][:, cols],
-                op=ADD,
-            )
-            nc.sync.dma_start(out=out[b * P : (b + 1) * P, cols], in_=result[b][:, cols])
-
         def finish(b, s):
             cols = span((s,))
             nc.vector.tensor_tensor(
@@ -261,5 +251,4 @@ def tile_picked_grand_none_e_kernel(
         turn_back(1, 1)
         weigh(1, 3, both)
         finish(1, 0)
-        for t in range(SPAN // P):
-            finish_tile(1, 1, t)
+        finish(1, 1)

@@ -25,7 +25,7 @@ LIST = 16
 VT = V // P
 LAST_PLANE_LOADS = ((1280, 0), (1152, 0), (896, 896), (512, 320), (256, 0))
 PIECES = ((1, 0, 256, False), (1, 256, 256, False), (0, 0, 256, True), (0, 256, 128, False), (0, 384, 128, False))
-Y1_PIECES = ((1, 0, 256, 5), (1, 256, 256, 3), (0, 0, 512, 4))
+Y1_PIECES = ((1, 0, 256, 7), (1, 256, 256, 3), (0, 0, 512, 4))
 SPAN = V // 2
 
 
@@ -86,14 +86,14 @@ def tile_picked_grand_none_e_kernel(
         factor_rows = {}
         factor_banks = {}
         for d in range(D + 1):
-            spread = bank((0, 1, 2, 3)[d])
+            spread = bank((0, 5, 2, 6)[d])
             factor_banks[d] = spread
             for t in range(VT):
                 col = d * VT + t
                 nc.tensor.transpose(
                     spread[:, t * P : (t + 1) * P], factor[:, col : col + 1].to_broadcast([P, P]), ident[:]
                 )
-            if d in (0, 1, 2, 3,):
+            if d in (0, 2,):
                 factor_rows[d] = keep.tile([P, V], F32, name="factor_row%d" % d)
                 nc.scalar.activation(out=factor_rows[d][:], in_=spread[:], func=COPY)
 
@@ -152,6 +152,7 @@ def tile_picked_grand_none_e_kernel(
         added = {unit: 0 for unit in sums}
         terms = {(b, d): keep.tile([P, V], F32, name="term%d%d" % (b, d)) for b in range(2) for d in range(D + 1)}
         plains = {}
+        closing = {}
         result = [keep.tile([P, V], F32, name="result%d" % b) for b in range(2)]
         both, low, high = (0, 1), (0,), (1,)
 
@@ -164,6 +165,8 @@ def tile_picked_grand_none_e_kernel(
 
         def add_turned(b, d, halves):
             if d == D:
+                for s in halves:
+                    closing[b, s] = terms[b, d]
                 return
             for s in halves:
                 for t in range(SPAN // P):
@@ -227,28 +230,30 @@ def tile_picked_grand_none_e_kernel(
         def finish(b, s):
             cols = span((s,))
             nc.vector.tensor_tensor(
-                out=result[b][:, cols], in0=sums[b, s][:, SPAN : 2 * SPAN], in1=terms[b, D][:, cols], op=ADD
+                out=result[b][:, cols], in0=sums[b, s][:, SPAN : 2 * SPAN], in1=closing[b, s][:, cols], op=ADD
             )
             nc.sync.dma_start(out=out[b * P : (b + 1) * P, cols], in_=result[b][:, cols])
 
         fused(0, 0, both)
         fetch(0, 1, both)
         fused(0, 2, both)
-        weigh(0, 1, both)
+        weigh_from_bank(0, 1, both)
         fetch(0, 3, both)
         fused(1, 0, both)
         fetch(1, 1, both)
         turn_back(0, 0)
-        turn_back(0, 1)
-        fused(1, 2, both)
-        weigh(1, 1, both)
-        terms[0, 3] = plains[1, 1]
-        weigh(0, 3, both)
+        fused(1, 2, low)
+        fused(1, 2, high)
+        weigh_from_bank(1, 1, low)
+        weigh_from_bank(1, 1, high)
         fetch(1, 3, both)
-        finish(0, 0)
-        finish(0, 1)
+        turn_back(0, 1)
+        terms[0, 3] = plains[1, 1]
+        weigh_from_bank(0, 3, both)
         turn_back(1, 0)
         turn_back(1, 1)
-        weigh(1, 3, both)
+        weigh_from_bank(1, 3, both)
+        finish(0, 0)
+        finish(0, 1)
         finish(1, 0)
         finish(1, 1)

@@ -23,10 +23,16 @@ PACK = 4
 HALF = S // 2
 LIST = 16
 VT = V // P
+SPAN = V // 2
+LOW, HIGH, ALL = slice(0, SPAN), slice(SPAN, V), slice(0, V)
+ADDED = (0, 2, 1)
+CLOSING = 3
+
 LAST_PLANE_LOADS = ((1280, 0), (1152, 0), (896, 896), (512, 320), (256, 0))
 PIECES = ((1, 0, 256, False), (1, 256, 256, False), (0, 0, 256, True), (0, 256, 128, False), (0, 384, 128, False))
-Y1_PIECES = ((1, 0, 256, 7), (1, 256, 256, 3), (0, 0, 512, 4))
-SPAN = V // 2
+LATER_PIECES = ((1, 0, 256, 7), (1, 256, 256, 3), (0, 0, 512, 4))
+WEIGHT_BANKS = (0, 5, 2, 6)
+GATE_BANK = 4
 
 
 def tile_picked_grand_none_e_kernel(
@@ -54,9 +60,9 @@ def tile_picked_grand_none_e_kernel(
         planes = [keep.tile([P, T], F32, name="plane%d" % j) for j in range(PACK)]
         nc.sync.dma_start(out=planes[0][:], in_=rows[:, 0, :])
         nc.sync.dma_start(offs_sb[:], offs)
-        gate_flat = gate.rearrange("d r (t p) -> (d r t) p", p=P)
+        gate_runs = gate.rearrange("d r (t p) -> (d r t) p", p=P)
         stride = P + 1
-        nc.sync.dma_start(out=gate_rows[0 : D * VT, :], in_=gate_flat[0 : (D * VT - 1) * stride + 1 : stride, :])
+        nc.sync.dma_start(out=gate_rows[0 : D * VT, :], in_=gate_runs[0 : (D * VT - 1) * stride + 1 : stride, :])
         for j in range(1, PACK - 1):
             nc.sync.dma_start(out=planes[j][:], in_=rows[:, j, :])
         last_plane = planes[PACK - 1]
@@ -70,32 +76,35 @@ def tile_picked_grand_none_e_kernel(
             nc.sync.dma_start(
                 out=w_scale[32 * q : 32 * q + 4, :].bitcast(I32), in_=w1_scales[0, 4 * q : 4 * q + 4, :].bitcast(I32)
             )
-        for tile_, src in zip(lists, (cen, pos1, pos2, pos3)):
-            nc.sync.dma_start(tile_[:], src)
+        for list_sb, src in zip(lists, (cen, pos1, pos2, pos3)):
+            nc.sync.dma_start(list_sb[:], src)
 
-        gate_t = bank(4)
-        nc.tensor.transpose(gate_t[:, 0:P], gate_rows[:], ident[:])
-        factor = keep.tile([P, (D + 1) * VT], F32, name="factor")
+        gate_turned = bank(GATE_BANK)
+        nc.tensor.transpose(gate_turned[:, 0:P], gate_rows[:], ident[:])
+        weight = keep.tile([P, (D + 1) * VT], F32, name="weight")
         gate_sum = keep.tile([P, VT], F32, name="gate_sum")
-        nc.vector.tensor_copy(out=factor[:, VT:], in_=gate_t[:, 0 : D * VT])
+        nc.vector.tensor_copy(out=weight[:, VT:], in_=gate_turned[:, 0 : D * VT])
         nc.vector.tensor_reduce(
-            out=gate_sum[:], in_=gate_t[:, 0 : D * VT].rearrange("p (d t) -> p t d", d=D), axis=mybir.AxisListType.X, op=ADD
+            out=gate_sum[:],
+            in_=gate_turned[:, 0 : D * VT].rearrange("p (d t) -> p t d", d=D),
+            axis=mybir.AxisListType.X,
+            op=ADD,
         )
-        nc.vector.tensor_scalar(out=factor[:, 0:VT], in0=gate_sum[:], scalar1=-1.0, scalar2=1.0, op0=MULT, op1=ADD)
+        nc.vector.tensor_scalar(out=weight[:, 0:VT], in0=gate_sum[:], scalar1=-1.0, scalar2=1.0, op0=MULT, op1=ADD)
 
-        factor_rows = {}
-        factor_banks = {}
-        for d in range(D + 1):
-            spread = bank((0, 5, 2, 6)[d])
-            factor_banks[d] = spread
+        weight_bank = []
+        weight_row = {}
+        for d, kept in enumerate((ALL, None, ALL, LOW)):
+            spread = bank(WEIGHT_BANKS[d])
             for t in range(VT):
                 col = d * VT + t
                 nc.tensor.transpose(
-                    spread[:, t * P : (t + 1) * P], factor[:, col : col + 1].to_broadcast([P, P]), ident[:]
+                    spread[:, t * P : (t + 1) * P], weight[:, col : col + 1].to_broadcast([P, P]), ident[:]
                 )
-            if d in (0, 2,):
-                factor_rows[d] = keep.tile([P, V], F32, name="factor_row%d" % d)
-                nc.scalar.activation(out=factor_rows[d][:], in_=spread[:], func=COPY)
+            weight_bank.append(spread)
+            if kept is not None:
+                weight_row[d] = keep.tile([P, kept.stop], F32, name="weight_row%d" % d)
+                nc.scalar.activation(out=weight_row[d][:], in_=spread[:, kept], func=COPY)
 
         grouped = [keep.tile([P, HALF, PACK], BF16, name="grouped%d" % h, align_bytes=64) for h in range(2)]
         half_offs = [offs_sb[:, h * HALF // LIST : (h + 1) * HALF // LIST] for h in range(2)]
@@ -118,142 +127,109 @@ def tile_picked_grand_none_e_kernel(
         scales = [keep.tile([P, HALF], U8, name="scales%d" % h, align_bytes=64) for h in range(2)]
         y = [keep.tile([P, S], F32, name="y%d" % b) for b in range(2)]
 
-        def product(b, h, cols, on_vector, number):
+        def product(b, h, first, count, on_vector, number):
             acc = bank(number)
-            width = cols.stop - cols.start
             nc.tensor.matmul_mx(
-                out=acc[:, 0:width],
+                out=acc[:, 0:count],
                 lhsT=w_codes[:, 2 * P * b : 2 * P * (b + 1)].bitcast(FP4X4),
                 lhsT_scale=w_scale[:, P * b : P * (b + 1)],
-                rhs=codes[h][:, cols].bitcast(FP8X4),
-                rhs_scale=scales[h][:, cols],
+                rhs=codes[h][:, first : first + count].bitcast(FP8X4),
+                rhs_scale=scales[h][:, first : first + count],
                 start=True,
                 stop=True,
             )
-            dst = y[b][:, h * HALF + cols.start : h * HALF + cols.stop]
+            dst = y[b][:, h * HALF + first : h * HALF + first + count]
             if on_vector:
-                nc.vector.tensor_copy(out=dst, in_=acc[:, 0:width])
+                nc.vector.tensor_copy(out=dst, in_=acc[:, 0:count])
             else:
-                nc.scalar.activation(out=dst, in_=acc[:, 0:width], func=COPY)
+                nc.scalar.activation(out=dst, in_=acc[:, 0:count], func=COPY)
 
-        for i, (h, first, count, on_vector) in enumerate(PIECES):
-            cols = slice(first, first + count)
+        for number, (h, first, count, on_vector) in enumerate(PIECES):
             flat = grouped[h][:].rearrange("p n j -> p (n j)")
             nc.vector.quantize_mx(
-                out=codes[h][:, cols].bitcast(FP8X4),
-                scales=scales[h][:, cols],
-                in_=flat[:, PACK * cols.start : PACK * cols.stop],
+                out=codes[h][:, first : first + count].bitcast(FP8X4),
+                scales=scales[h][:, first : first + count],
+                in_=flat[:, PACK * first : PACK * (first + count)],
             )
-            product(0, h, cols, on_vector, i)
-        for h, first, count, number in Y1_PIECES:
-            product(1, h, slice(first, first + count), False, number)
+            product(0, h, first, count, on_vector, number)
+        for h, first, count, number in LATER_PIECES:
+            product(1, h, first, count, False, number)
 
-        sums = {(b, s): bank(2 * b + s) for b in range(2) for s in range(2)}
-        added = {unit: 0 for unit in sums}
-        terms = {(b, d): keep.tile([P, V], F32, name="term%d%d" % (b, d)) for b in range(2) for d in range(D + 1)}
-        plains = {}
-        closing = {}
+        sums = {(b, cols.start): bank(2 * b + cols.start // SPAN) for b in range(2) for cols in (LOW, HIGH)}
         result = [keep.tile([P, V], F32, name="result%d" % b) for b in range(2)]
-        both, low, high = (0, 1), (0,), (1,)
 
-        def span(halves):
-            return slice(halves[0] * SPAN, (halves[-1] + 1) * SPAN)
+        def wide_tile(name):
+            return keep.tile([P, V], F32, name=name)
 
-        def lookup(b, d, halves):
-            cols = span(halves)
+        def look_up(b, d, cols):
             return y[b][:].indirect(lists[d][:, cols.start // LIST : cols.stop // LIST])
 
-        def add_turned(b, d, halves):
-            if d == D:
-                for s in halves:
-                    closing[b, s] = terms[b, d]
-                return
-            for s in halves:
-                for t in range(SPAN // P):
-                    first = s * SPAN + t * P
-                    nc.tensor.matmul(
-                        sums[b, s][:, t * P : (t + 1) * P],
-                        lhsT=terms[b, d][:, first : first + P],
-                        rhs=ident[:],
-                        is_transpose=True,
-                        start=added[b, s] == 0 and t == 0,
-                        stop=added[b, s] == D - 1 and t == SPAN // P - 1,
-                    )
-                added[b, s] = added[b, s] + 1
-
-        def fused(b, d, halves):
-            cols = span(halves)
-            nc.vector.tensor_tensor(
-                out=terms[b, d][:, cols], in0=lookup(b, d, halves), in1=factor_rows[d][:, cols], op=MULT
-            )
-            add_turned(b, d, halves)
-
-        def fetch(b, d, halves):
-            if (b, d) not in plains:
-                plains[b, d] = keep.tile([P, V], F32, name="plain%d%d" % (b, d))
-            nc.scalar.activation(out=plains[b, d][:, span(halves)], in_=lookup(b, d, halves), func=COPY)
-
-        def fetch_on_vector(b, d, halves):
-            if (b, d) not in plains:
-                plains[b, d] = keep.tile([P, V], F32, name="plain%d%d" % (b, d))
-            nc.vector.tensor_copy(out=plains[b, d][:, span(halves)], in_=lookup(b, d, halves))
-
-        def weigh_on_gpsimd(b, d, halves):
-            cols = span(halves)
-            nc.gpsimd.tensor_tensor(
-                out=terms[b, d][:, cols], in0=plains[b, d][:, cols], in1=factor_rows[d][:, cols], op=MULT
-            )
-            add_turned(b, d, halves)
-
-        def weigh_from_bank(b, d, halves):
-            cols = span(halves)
-            nc.vector.tensor_tensor(
-                out=terms[b, d][:, cols], in0=plains[b, d][:, cols], in1=factor_banks[d][:, cols], op=MULT
-            )
-            add_turned(b, d, halves)
-
-        def weigh(b, d, halves):
-            cols = span(halves)
-            nc.vector.tensor_tensor(
-                out=terms[b, d][:, cols], in0=plains[b, d][:, cols], in1=factor_rows[d][:, cols], op=MULT
-            )
-            add_turned(b, d, halves)
-
-        def turn_back(b, s):
-            staged = keep.tile([P, SPAN], F32, name="staged%d%d" % (b, s))
-            nc.scalar.activation(out=staged[:], in_=sums[b, s][:, 0:SPAN], func=COPY)
-            for t in range(SPAN // P):
-                nc.tensor.transpose(
-                    sums[b, s][:, SPAN + t * P : SPAN + (t + 1) * P], staged[:, t * P : (t + 1) * P], ident[:]
+        def add_turned(b, d, term, cols):
+            for first in range(cols.start, cols.stop, P):
+                at = first % SPAN
+                nc.tensor.matmul(
+                    sums[b, first - at][:, at : at + P],
+                    lhsT=term[:, first : first + P],
+                    rhs=ident[:],
+                    is_transpose=True,
+                    start=d == ADDED[0] and at == 0,
+                    stop=d == ADDED[-1] and at == SPAN - P,
                 )
 
-        def finish(b, s):
-            cols = span((s,))
+        def fused(b, d, term, cols):
+            nc.vector.tensor_tensor(out=term[:, cols], in0=look_up(b, d, cols), in1=weight_row[d][:, cols], op=MULT)
+            add_turned(b, d, term, cols)
+
+        def fetch(b, d):
+            plain = wide_tile("plain%d%d" % (b, d))
+            nc.scalar.activation(out=plain[:], in_=look_up(b, d, ALL), func=COPY)
+            return plain
+
+        def weigh(d, term, plain, cols):
+            nc.vector.tensor_tensor(out=term[:, cols], in0=plain[:, cols], in1=weight_bank[d][:, cols], op=MULT)
+
+        def turn_back(b, cols):
+            total = sums[b, cols.start]
+            staged = keep.tile([P, SPAN], F32, name="staged%d_%d" % (b, cols.start))
+            nc.scalar.activation(out=staged[:], in_=total[:, 0:SPAN], func=COPY)
+            for at in range(0, SPAN, P):
+                nc.tensor.transpose(total[:, SPAN + at : SPAN + at + P], staged[:, at : at + P], ident[:])
+
+        def finish(b, closing, cols):
             nc.vector.tensor_tensor(
-                out=result[b][:, cols], in0=sums[b, s][:, SPAN : 2 * SPAN], in1=closing[b, s][:, cols], op=ADD
+                out=result[b][:, cols], in0=sums[b, cols.start][:, SPAN:V], in1=closing[:, cols], op=ADD
             )
             nc.sync.dma_start(out=out[b * P : (b + 1) * P, cols], in_=result[b][:, cols])
 
-        fused(0, 0, both)
-        fetch(0, 1, both)
-        fused(0, 2, both)
-        weigh_from_bank(0, 1, both)
-        fetch(0, 3, both)
-        fused(1, 0, both)
-        fetch(1, 1, both)
-        turn_back(0, 0)
-        fused(1, 2, low)
-        fused(1, 2, high)
-        weigh_from_bank(1, 1, low)
-        weigh_from_bank(1, 1, high)
-        fetch(1, 3, both)
-        turn_back(0, 1)
-        terms[0, 3] = plains[1, 1]
-        weigh_from_bank(0, 3, both)
-        turn_back(1, 0)
-        turn_back(1, 1)
-        weigh_from_bank(1, 3, both)
-        finish(0, 0)
-        finish(0, 1)
-        finish(1, 0)
-        finish(1, 1)
+        term = {(b, d): wide_tile("term%d%d" % (b, d)) for b in range(2) for d in ADDED}
+
+        fused(0, 0, term[0, 0], ALL)
+        plain01 = fetch(0, 1)
+        fused(0, 2, term[0, 2], ALL)
+        weigh(1, term[0, 1], plain01, ALL)
+        add_turned(0, 1, term[0, 1], ALL)
+        plain03 = fetch(0, CLOSING)
+
+        fused(1, 0, term[1, 0], ALL)
+        plain11 = fetch(1, 1)
+        turn_back(0, LOW)
+        for cols in (LOW, HIGH):
+            fused(1, 2, term[1, 2], cols)
+        nc.gpsimd.tensor_tensor(
+            out=term[1, 2][:, LOW], in0=plain03[:, LOW], in1=weight_row[CLOSING][:, LOW], op=MULT
+        )
+        for cols in (LOW, HIGH):
+            weigh(1, term[1, 1], plain11, cols)
+            add_turned(1, 1, term[1, 1], cols)
+
+        plain13 = fetch(1, CLOSING)
+        turn_back(0, HIGH)
+        weigh(CLOSING, plain11, plain03, HIGH)
+        for cols in (LOW, HIGH):
+            turn_back(1, cols)
+        closing1 = wide_tile("closing1")
+        weigh(CLOSING, closing1, plain13, ALL)
+        finish(0, term[1, 2], LOW)
+        finish(0, plain11, HIGH)
+        for cols in (LOW, HIGH):
+            finish(1, closing1, cols)

@@ -28,7 +28,8 @@ LOW, HIGH, ALL = slice(0, SPAN), slice(SPAN, V), slice(0, V)
 ADDED = (0, 2, 1)
 CLOSING = 3
 
-LAST_PLANE_LOADS = ((1280, 0), (1152, 0), (896, 896), (512, 320), (256, 0))
+LAID_BY_SCALAR = ((128, 128), (256, 128), (384, 128))
+LAID_BY_VECTOR = (0, 128)
 PIECES = ((1, 0, 256, False), (1, 256, 256, False), (0, 0, 256, True), (0, 256, 128, False), (0, 384, 128, False))
 LATER_PIECES = ((1, 0, 256, 7), (1, 256, 256, 3), (0, 0, 512, 4))
 WEIGHT_BANKS = (0, 5, 2, 6)
@@ -57,19 +58,15 @@ def tile_picked_grand_none_e_kernel(
         make_identity(nc, ident[:])
 
         rows = xT.rearrange("(p j) t -> p j t", j=PACK)
-        planes = [keep.tile([P, T], F32, name="plane%d" % j) for j in range(PACK)]
+        planes = [keep.tile([P, T], F32, name="plane%d" % j, tag="plane%d" % j) for j in range(PACK)]
         nc.sync.dma_start(out=planes[0][:], in_=rows[:, 0, :])
         nc.sync.dma_start(offs_sb[:], offs)
         gate_runs = gate.rearrange("d r (t p) -> (d r t) p", p=P)
         stride = P + 1
         nc.sync.dma_start(out=gate_rows[0 : D * VT, :], in_=gate_runs[0 : (D * VT - 1) * stride + 1 : stride, :])
-        for j in range(1, PACK - 1):
+        for j in range(1, PACK):
             nc.sync.dma_start(out=planes[j][:], in_=rows[:, j, :])
         last_plane = planes[PACK - 1]
-        c0 = 0
-        for width, on_vector in LAST_PLANE_LOADS:
-            nc.sync.dma_start(out=last_plane[:, c0 : c0 + width], in_=rows[:, PACK - 1, c0 : c0 + width])
-            c0 = c0 + width
         w_codes = keep.tile([P, 2 * N], U8, name="w_codes", align_bytes=64)
         nc.sync.dma_start(out=w_codes[:], in_=w1_words[0])
         for q in range(4):
@@ -111,17 +108,18 @@ def tile_picked_grand_none_e_kernel(
         for j in range(PACK - 1):
             for h in range(2):
                 nc.vector.tensor_copy(out=grouped[h][:, :, j], in_=planes[j][:].indirect(half_offs[h]))
-        last_bf = keep.tile([P, T], BF16, name="last_bf")
-        c0 = 0
-        for width, on_vector in LAST_PLANE_LOADS:
-            split = c0 + on_vector
-            if on_vector > 0:
-                nc.vector.tensor_copy(out=last_bf[:, c0:split], in_=last_plane[:, c0:split])
-            if on_vector < width:
-                nc.scalar.activation(out=last_bf[:, split : c0 + width], in_=last_plane[:, split : c0 + width], func=COPY)
-            c0 = c0 + width
+        dense = keep.tile([P, HALF], BF16, name="dense", tag="plane%d" % (PACK - 2))
         nc.vector.tensor_copy(out=grouped[1][:, :, PACK - 1], in_=last_plane[:].indirect(half_offs[1]))
-        nc.scalar.activation(out=grouped[0][:, :, PACK - 1], in_=last_bf[:].indirect(half_offs[0]), func=COPY)
+        for first, count in ((0, HALF // 2), (HALF // 2, HALF // 2)):
+            nc.scalar.activation(
+                out=dense[:, first : first + count],
+                in_=last_plane[:].indirect(offs_sb[:, first // LIST : (first + count) // LIST]),
+                func=COPY,
+            )
+        first, count = LAID_BY_VECTOR
+        nc.vector.tensor_copy(out=grouped[0][:, first : first + count, PACK - 1], in_=dense[:, first : first + count])
+        for first, count in LAID_BY_SCALAR:
+            nc.scalar.copy(out=grouped[0][:, first : first + count, PACK - 1], in_=dense[:, first : first + count])
 
         codes = [keep.tile([P, HALF], U32, name="codes%d" % h, align_bytes=64) for h in range(2)]
         scales = [keep.tile([P, HALF], U8, name="scales%d" % h, align_bytes=64) for h in range(2)]

@@ -30,10 +30,11 @@ CLOSING = 3
 
 LAID_BY_SCALAR = ((128, 128), (256, 128), (384, 128))
 LAID_BY_VECTOR = (0, 128)
-PIECES = ((1, 0, 256, False), (1, 256, 256, False), (0, 0, 256, True), (0, 256, 128, False), (0, 384, 128, False))
-LATER_PIECES = ((1, 0, 256, 7), (1, 256, 256, 3), (0, 0, 512, 4))
+PIECES = ((1, 0, 128, False), (1, 128, 128, False), (1, 256, 256, False), (0, 0, 256, True), (0, 256, 128, False), (0, 384, 128, False))
+LATER_PIECES = ((1, 0, 256, 0), (1, 256, 256, 3), (0, 0, 512, 4))
 WEIGHT_BANKS = (0, 5, 2, 6)
 GATE_BANK = 4
+PIECE_BANKS = (0, 7, 1, 2, 3, 4)
 
 
 def tile_picked_grand_none_e_kernel(
@@ -142,7 +143,7 @@ def tile_picked_grand_none_e_kernel(
             else:
                 nc.scalar.activation(out=dst, in_=acc[:, 0:count], func=COPY)
 
-        for number, (h, first, count, on_vector) in enumerate(PIECES):
+        for number, (h, first, count, on_vector) in zip(PIECE_BANKS, PIECES):
             flat = grouped[h][:].rearrange("p n j -> p (n j)")
             nc.vector.quantize_mx(
                 out=codes[h][:, first : first + count].bitcast(FP8X4),

@@ -28,9 +28,9 @@ LOW, HIGH, ALL = slice(0, SPAN), slice(SPAN, V), slice(0, V)
 ADDED = (0, 2, 1)
 CLOSING = 3
 
-LAID_BY_SCALAR = ((128, 128), (256, 128), (384, 128))
-LAID_BY_VECTOR = (0, 128)
-PIECES = ((1, 0, 128, False), (1, 128, 128, False), (1, 256, 256, False), (0, 0, 256, True), (0, 256, 128, False), (0, 384, 128, False))
+LAID_BY_GPSIMD = ((0, 128), (128, 128))
+LAID_BY_SCALAR = ((256, 128), (384, 128))
+PIECES = ((0, 0, 128, False), (0, 128, 128, False), (1, 0, 256, False), (1, 256, 256, True), (0, 256, 128, False), (0, 384, 128, False))
 LATER_PIECES = ((1, 0, 256, 0), (1, 256, 256, 3), (0, 0, 512, 4))
 WEIGHT_BANKS = (0, 5, 2, 6)
 GATE_BANK = 4
@@ -59,7 +59,7 @@ def tile_picked_grand_none_e_kernel(
         make_identity(nc, ident[:])
 
         rows = xT.rearrange("(p j) t -> p j t", j=PACK)
-        planes = [keep.tile([P, T], F32, name="plane%d" % j, tag="plane%d" % j) for j in range(PACK)]
+        planes = [keep.tile([P, T], F32, name="plane%d" % j, tag="plane%d" % j, align_bytes=64) for j in range(PACK)]
         nc.sync.dma_start(out=planes[0][:], in_=rows[:, 0, :])
         nc.sync.dma_start(offs_sb[:], offs)
         gate_runs = gate.rearrange("d r (t p) -> (d r t) p", p=P)
@@ -109,20 +109,30 @@ def tile_picked_grand_none_e_kernel(
         for j in range(PACK - 1):
             for h in range(2):
                 nc.vector.tensor_copy(out=grouped[h][:, :, j], in_=planes[j][:].indirect(half_offs[h]))
-        dense = keep.tile([P, HALF], BF16, name="dense", tag="plane%d" % (PACK - 2))
+        quarter = HALF // 2
+        dense_g = keep.tile([P, quarter], BF16, name="dense_g", tag="plane%d" % (PACK - 2), align_bytes=64)
+        dense_s = keep.tile([P, quarter], BF16, name="dense_s")
         nc.vector.tensor_copy(out=grouped[1][:, :, PACK - 1], in_=last_plane[:].indirect(half_offs[1]))
-        for first, count in ((0, HALF // 2), (HALF // 2, HALF // 2)):
+        for first, count in LAID_BY_GPSIMD:
             nc.scalar.activation(
-                out=dense[:, first : first + count],
+                out=dense_g[:, first : first + count],
                 in_=last_plane[:].indirect(offs_sb[:, first // LIST : (first + count) // LIST]),
                 func=COPY,
             )
-        first, count = LAID_BY_VECTOR
-        nc.vector.tensor_copy(out=grouped[0][:, first : first + count, PACK - 1], in_=dense[:, first : first + count])
+            nc.gpsimd.tensor_copy(out=grouped[0][:, first : first + count, PACK - 1], in_=dense_g[:, first : first + count])
+        nc.scalar.activation(
+            out=dense_s[:], in_=last_plane[:].indirect(offs_sb[:, quarter // LIST : HALF // LIST]), func=COPY
+        )
         for first, count in LAID_BY_SCALAR:
-            nc.scalar.copy(out=grouped[0][:, first : first + count, PACK - 1], in_=dense[:, first : first + count])
+            nc.scalar.copy(
+                out=grouped[0][:, first : first + count, PACK - 1],
+                in_=dense_s[:, first - quarter : first - quarter + count],
+            )
 
-        codes = [keep.tile([P, HALF], U32, name="codes%d" % h, align_bytes=64) for h in range(2)]
+        codes = [
+            keep.tile([P, HALF], U32, name="codes0", align_bytes=64),
+            keep.tile([P, HALF], U32, name="codes1", tag="plane%d" % (PACK - 2), align_bytes=64),
+        ]
         scales = [keep.tile([P, HALF], U8, name="scales%d" % h, align_bytes=64) for h in range(2)]
         y = [keep.tile([P, S], F32, name="y%d" % b) for b in range(2)]
 

@@ -197,12 +197,18 @@ def tile_picked_grand_none_e_kernel(
         def weigh(d, term, plain, cols):
             nc.vector.tensor_tensor(out=term[:, cols], in0=plain[:, cols], in1=weight_bank[d][:, cols], op=MULT)
 
-        def turn_back(b, cols):
-            total = sums[b, cols.start]
+        def copy_out(b, cols):
             staged = keep.tile([P, SPAN], F32, name="staged%d_%d" % (b, cols.start))
-            nc.scalar.activation(out=staged[:], in_=total[:, 0:SPAN], func=COPY)
+            nc.scalar.activation(out=staged[:], in_=sums[b, cols.start][:, 0:SPAN], func=COPY)
+            return staged
+
+        def turn(b, cols, staged):
+            total = sums[b, cols.start]
             for at in range(0, SPAN, P):
                 nc.tensor.transpose(total[:, SPAN + at : SPAN + at + P], staged[:, at : at + P], ident[:])
+
+        def turn_back(b, cols):
+            turn(b, cols, copy_out(b, cols))
 
         def finish(b, closing, cols):
             nc.vector.tensor_tensor(
@@ -221,9 +227,10 @@ def tile_picked_grand_none_e_kernel(
 
         fused(1, 0, term[1, 0], ALL)
         plain11 = fetch(1, 1)
-        turn_back(0, LOW)
-        for cols in (LOW, HIGH):
-            fused(1, 2, term[1, 2], cols)
+        staged0 = copy_out(0, LOW)
+        fused(1, 2, term[1, 2], LOW)
+        turn(0, LOW, staged0)
+        fused(1, 2, term[1, 2], HIGH)
         nc.gpsimd.tensor_tensor(
             out=term[1, 2][:, LOW], in0=plain03[:, LOW], in1=weight_row[CLOSING][:, LOW], op=MULT
         )

@@ -189,17 +189,19 @@ def tile_picked_grand_none_e_kernel(
             nc.vector.tensor_tensor(out=term[:, cols], in0=look_up(b, d, cols), in1=weight_row[d][:, cols], op=MULT)
             add_turned(b, d, term, cols)
 
-        def fetch(b, d):
-            plain = wide_tile("plain%d%d" % (b, d))
-            nc.scalar.activation(out=plain[:], in_=look_up(b, d, ALL), func=COPY)
+        def fetch(b, d, plain=None):
+            if plain is None:
+                plain = wide_tile("plain%d%d" % (b, d))[:]
+            nc.scalar.activation(out=plain, in_=look_up(b, d, ALL), func=COPY)
             return plain
 
         def weigh(d, term, plain, cols):
             nc.vector.tensor_tensor(out=term[:, cols], in0=plain[:, cols], in1=weight_bank[d][:, cols], op=MULT)
 
-        def copy_out(b, cols):
-            staged = keep.tile([P, SPAN], F32, name="staged%d_%d" % (b, cols.start))
-            nc.scalar.activation(out=staged[:], in_=sums[b, cols.start][:, 0:SPAN], func=COPY)
+        def copy_out(b, cols, staged=None):
+            if staged is None:
+                staged = keep.tile([P, SPAN], F32, name="staged%d_%d" % (b, cols.start))[:]
+            nc.scalar.activation(out=staged, in_=sums[b, cols.start][:, 0:SPAN], func=COPY)
             return staged
 
         def turn(b, cols, staged):
@@ -212,7 +214,7 @@ def tile_picked_grand_none_e_kernel(
 
         def finish(b, closing, cols):
             nc.vector.tensor_tensor(
-                out=result[b][:, cols], in0=sums[b, cols.start][:, SPAN:V], in1=closing[:, cols], op=ADD
+                out=result[b][:, cols], in0=sums[b, cols.start][:, SPAN:V], in1=closing, op=ADD
             )
             nc.sync.dma_start(out=out[b * P : (b + 1) * P, cols], in_=result[b][:, cols])
 
@@ -227,12 +229,13 @@ def tile_picked_grand_none_e_kernel(
 
         fused(1, 0, term[1, 0], ALL)
         plain11 = fetch(1, 1)
-        staged0 = copy_out(0, LOW)
+        closing1 = wide_tile("closing1")
+        staged0 = copy_out(0, LOW, closing1[:, LOW])
         fused(1, 2, term[1, 2], LOW)
         turn(0, LOW, staged0)
         fused(1, 2, term[1, 2], HIGH)
         nc.gpsimd.tensor_tensor(
-            out=term[1, 2][:, LOW], in0=plain03[:, LOW], in1=weight_row[CLOSING][:, LOW], op=MULT
+            out=weight_row[2][:, LOW], in0=plain03[:, LOW], in1=weight_row[CLOSING][:, LOW], op=MULT
         )
         for cols in (LOW, HIGH):
             weigh(1, term[1, 1], plain11, cols)
@@ -240,12 +243,11 @@ def tile_picked_grand_none_e_kernel(
 
         plain13 = fetch(1, CLOSING)
         turn_back(0, HIGH)
-        weigh(CLOSING, plain11, plain03, HIGH)
+        nc.vector.tensor_tensor(out=plain11[:, LOW], in0=plain03[:, HIGH], in1=weight_bank[CLOSING][:, HIGH], op=MULT)
         for cols in (LOW, HIGH):
             turn_back(1, cols)
-        closing1 = wide_tile("closing1")
+        finish(0, weight_row[2][:, LOW], LOW)
         weigh(CLOSING, closing1, plain13, ALL)
-        finish(0, term[1, 2], LOW)
-        finish(0, plain11, HIGH)
+        finish(0, plain11[:, LOW], HIGH)
         for cols in (LOW, HIGH):
-            finish(1, closing1, cols)
+            finish(1, closing1[:, cols], cols)

@@ -242,12 +242,13 @@ def tile_picked_grand_none_e_kernel(
             add_turned(1, 1, term[1, 1], cols)
 
         plain13 = fetch(1, CLOSING)
-        turn_back(0, HIGH)
-        nc.vector.tensor_tensor(out=plain11[:, LOW], in0=plain03[:, HIGH], in1=weight_bank[CLOSING][:, HIGH], op=MULT)
+        nc.vector.tensor_copy(out=plain11[:, LOW], in_=sums[0, HIGH.start][:, 0:SPAN])
+        turn(0, HIGH, plain11[:, LOW])
+        weigh(CLOSING, plain11, plain03, HIGH)
         for cols in (LOW, HIGH):
             turn_back(1, cols)
         finish(0, weight_row[2][:, LOW], LOW)
         weigh(CLOSING, closing1, plain13, ALL)
-        finish(0, plain11[:, LOW], HIGH)
+        finish(0, plain11[:, HIGH], HIGH)
         for cols in (LOW, HIGH):
             finish(1, closing1[:, cols], cols)

@@ -21,20 +21,29 @@ ADD = mybir.AluOpType.add
 P = 128
 PACK = 4
 HALF = S // 2
+QUARTER = S // 4
 LIST = 16
 VT = V // P
 SPAN = V // 2
 LOW, HIGH, ALL = slice(0, SPAN), slice(SPAN, V), slice(0, V)
+FRONT, BACK = slice(0, V - P), slice(V - P, V)
 ADDED = (0, 2, 1)
 CLOSING = 3
 
 LAID_BY_GPSIMD = ((0, 128), (128, 128))
 LAID_BY_SCALAR = ((256, 128), (384, 128))
-PIECES = ((0, 0, 128, False), (0, 128, 128, False), (1, 0, 256, False), (1, 256, 256, True), (0, 256, 128, False), (0, 384, 128, False))
+PIECES = (
+    (0, 0, 128, False),
+    (0, 128, 128, False),
+    (1, 0, 256, False),
+    (1, 256, 256, True),
+    (0, 256, 128, False),
+    (0, 384, 128, False),
+)
+PIECE_BANKS = (0, 7, 1, 2, 3, 4)
 LATER_PIECES = ((1, 0, 256, 0), (1, 256, 256, 3), (0, 0, 512, 4))
 WEIGHT_BANKS = (0, 5, 2, 6)
 GATE_BANK = 4
-PIECE_BANKS = (0, 7, 1, 2, 3, 4)
 
 
 def tile_picked_grand_none_e_kernel(
@@ -59,7 +68,9 @@ def tile_picked_grand_none_e_kernel(
         make_identity(nc, ident[:])
 
         rows = xT.rearrange("(p j) t -> p j t", j=PACK)
-        planes = [keep.tile([P, T], F32, name="plane%d" % j, tag="plane%d" % j, align_bytes=64) for j in range(PACK)]
+        planes = [
+            keep.tile([P, T], F32, name="plane%d" % j, tag="plane%d" % j, align_bytes=64) for j in range(PACK)
+        ]
         nc.sync.dma_start(out=planes[0][:], in_=rows[:, 0, :])
         nc.sync.dma_start(offs_sb[:], offs)
         gate_runs = gate.rearrange("d r (t p) -> (d r t) p", p=P)
@@ -92,7 +103,7 @@ def tile_picked_grand_none_e_kernel(
 
         weight_bank = []
         weight_row = {}
-        for d, kept in enumerate((ALL, None, ALL, LOW)):
+        for d, kept in enumerate((ALL, BACK, ALL, LOW)):
             spread = bank(WEIGHT_BANKS[d])
             for t in range(VT):
                 col = d * VT + t
@@ -100,18 +111,16 @@ def tile_picked_grand_none_e_kernel(
                     spread[:, t * P : (t + 1) * P], weight[:, col : col + 1].to_broadcast([P, P]), ident[:]
                 )
             weight_bank.append(spread)
-            if kept is not None:
-                weight_row[d] = keep.tile([P, kept.stop], F32, name="weight_row%d" % d)
-                nc.scalar.activation(out=weight_row[d][:], in_=spread[:, kept], func=COPY)
+            weight_row[d] = keep.tile([P, kept.stop], F32, name="weight_row%d" % d)
+            nc.scalar.activation(out=weight_row[d][:, kept], in_=spread[:, kept], func=COPY)
 
         grouped = [keep.tile([P, HALF, PACK], BF16, name="grouped%d" % h, align_bytes=64) for h in range(2)]
         half_offs = [offs_sb[:, h * HALF // LIST : (h + 1) * HALF // LIST] for h in range(2)]
         for j in range(PACK - 1):
             for h in range(2):
                 nc.vector.tensor_copy(out=grouped[h][:, :, j], in_=planes[j][:].indirect(half_offs[h]))
-        quarter = HALF // 2
-        dense_g = keep.tile([P, quarter], BF16, name="dense_g", tag="plane%d" % (PACK - 2), align_bytes=64)
-        dense_s = keep.tile([P, quarter], BF16, name="dense_s")
+        dense_g = keep.tile([P, QUARTER], BF16, name="dense_g", tag="plane%d" % (PACK - 2), align_bytes=64)
+        dense_s = keep.tile([P, QUARTER], BF16, name="dense_s")
         nc.vector.tensor_copy(out=grouped[1][:, :, PACK - 1], in_=last_plane[:].indirect(half_offs[1]))
         for first, count in LAID_BY_GPSIMD:
             nc.scalar.activation(
@@ -119,14 +128,16 @@ def tile_picked_grand_none_e_kernel(
                 in_=last_plane[:].indirect(offs_sb[:, first // LIST : (first + count) // LIST]),
                 func=COPY,
             )
-            nc.gpsimd.tensor_copy(out=grouped[0][:, first : first + count, PACK - 1], in_=dense_g[:, first : first + count])
+            nc.gpsimd.tensor_copy(
+                out=grouped[0][:, first : first + count, PACK - 1], in_=dense_g[:, first : first + count]
+            )
         nc.scalar.activation(
-            out=dense_s[:], in_=last_plane[:].indirect(offs_sb[:, quarter // LIST : HALF // LIST]), func=COPY
+            out=dense_s[:], in_=last_plane[:].indirect(offs_sb[:, QUARTER // LIST : HALF // LIST]), func=COPY
         )
         for first, count in LAID_BY_SCALAR:
             nc.scalar.copy(
                 out=grouped[0][:, first : first + count, PACK - 1],
-                in_=dense_s[:, first - quarter : first - quarter + count],
+                in_=dense_s[:, first - QUARTER : first - QUARTER + count],
             )
 
         codes = [
@@ -189,20 +200,16 @@ def tile_picked_grand_none_e_kernel(
             nc.vector.tensor_tensor(out=term[:, cols], in0=look_up(b, d, cols), in1=weight_row[d][:, cols], op=MULT)
             add_turned(b, d, term, cols)
 
-        def fetch(b, d, plain=None):
-            if plain is None:
-                plain = wide_tile("plain%d%d" % (b, d))[:]
-            nc.scalar.activation(out=plain, in_=look_up(b, d, ALL), func=COPY)
+        def fetch(b, d):
+            plain = wide_tile("plain%d%d" % (b, d))
+            nc.scalar.activation(out=plain[:], in_=look_up(b, d, ALL), func=COPY)
             return plain
 
-        def weigh(d, term, plain, cols):
-            nc.vector.tensor_tensor(out=term[:, cols], in0=plain[:, cols], in1=weight_bank[d][:, cols], op=MULT)
+        def weigh(d, dst, plain, cols):
+            nc.vector.tensor_tensor(out=dst, in0=plain[:, cols], in1=weight_bank[d][:, cols], op=MULT)
 
-        def copy_out(b, cols, staged=None):
-            if staged is None:
-                staged = keep.tile([P, SPAN], F32, name="staged%d_%d" % (b, cols.start))[:]
+        def copy_out(b, cols, staged):
             nc.scalar.activation(out=staged, in_=sums[b, cols.start][:, 0:SPAN], func=COPY)
-            return staged
 
         def turn(b, cols, staged):
             total = sums[b, cols.start]
@@ -210,7 +217,9 @@ def tile_picked_grand_none_e_kernel(
                 nc.tensor.transpose(total[:, SPAN + at : SPAN + at + P], staged[:, at : at + P], ident[:])
 
         def turn_back(b, cols):
-            turn(b, cols, copy_out(b, cols))
+            staged = keep.tile([P, SPAN], F32, name="staged%d_%d" % (b, cols.start))
+            copy_out(b, cols, staged[:])
+            turn(b, cols, staged[:])
 
         def finish(b, closing, cols):
             nc.vector.tensor_tensor(
@@ -223,32 +232,33 @@ def tile_picked_grand_none_e_kernel(
         fused(0, 0, term[0, 0], ALL)
         plain01 = fetch(0, 1)
         fused(0, 2, term[0, 2], ALL)
-        weigh(1, term[0, 1], plain01, ALL)
+        weigh(1, term[0, 1][:, FRONT], plain01, FRONT)
+        nc.gpsimd.tensor_tensor(out=term[0, 1][:, BACK], in0=plain01[:, BACK], in1=weight_row[1][:, BACK], op=MULT)
         add_turned(0, 1, term[0, 1], ALL)
         plain03 = fetch(0, CLOSING)
 
         fused(1, 0, term[1, 0], ALL)
         plain11 = fetch(1, 1)
         closing1 = wide_tile("closing1")
-        staged0 = copy_out(0, LOW, closing1[:, LOW])
+        copy_out(0, LOW, closing1[:, LOW])
         fused(1, 2, term[1, 2], LOW)
-        turn(0, LOW, staged0)
+        turn(0, LOW, closing1[:, LOW])
         fused(1, 2, term[1, 2], HIGH)
-        nc.gpsimd.tensor_tensor(
-            out=weight_row[2][:, LOW], in0=plain03[:, LOW], in1=weight_row[CLOSING][:, LOW], op=MULT
-        )
+        closing0_low = weight_row[2][:, LOW]
+        nc.gpsimd.tensor_tensor(out=closing0_low, in0=plain03[:, LOW], in1=weight_row[CLOSING][:, LOW], op=MULT)
         for cols in (LOW, HIGH):
-            weigh(1, term[1, 1], plain11, cols)
+            weigh(1, term[1, 1][:, cols], plain11, cols)
             add_turned(1, 1, term[1, 1], cols)
 
         plain13 = fetch(1, CLOSING)
         nc.vector.tensor_copy(out=plain11[:, LOW], in_=sums[0, HIGH.start][:, 0:SPAN])
         turn(0, HIGH, plain11[:, LOW])
-        weigh(CLOSING, plain11, plain03, HIGH)
+        closing0_high = plain11[:, HIGH]
+        weigh(CLOSING, closing0_high, plain03, HIGH)
         for cols in (LOW, HIGH):
             turn_back(1, cols)
-        finish(0, weight_row[2][:, LOW], LOW)
-        weigh(CLOSING, closing1, plain13, ALL)
-        finish(0, plain11[:, HIGH], HIGH)
+        finish(0, closing0_low, LOW)
+        weigh(CLOSING, closing1[:], plain13, ALL)
+        finish(0, closing0_high, HIGH)
         for cols in (LOW, HIGH):
             finish(1, closing1[:, cols], cols)

from contextlib import ExitStack

import concourse.mybir as mybir
from concourse.masks import make_identity

K, T, S, D, V, N = 512, 4096, 1024, 3, 512, 256
FLOPS = 2 * K * N * S

F32 = mybir.dt.float32
BF16 = mybir.dt.bfloat16
I32 = mybir.dt.int32
U32 = mybir.dt.uint32
U16 = mybir.dt.uint16
U8 = mybir.dt.uint8
FP8X4 = mybir.dt.float8_e4m3fn_x4
FP4X4 = mybir.dt.float4_e2m1fn_x4
COPY = mybir.ActivationFunctionType.Copy
MULT = mybir.AluOpType.mult
ADD = mybir.AluOpType.add

P = 128
PACK = 4
HALF = S // 2
QUARTER = S // 4
LIST = 16
VT = V // P
SPAN = V // 2
LOW, HIGH, ALL = slice(0, SPAN), slice(SPAN, V), slice(0, V)
FRONT, BACK = slice(0, V - P), slice(V - P, V)
ADDED = (0, 2, 1)
CLOSING = 3

LAID_BY_GPSIMD = ((0, 128), (128, 128))
LAID_BY_SCALAR = ((256, 128), (384, 128))
PIECES = (
    (0, 0, 128, False),
    (0, 128, 128, False),
    (1, 0, 256, False),
    (1, 256, 256, True),
    (0, 256, 128, False),
    (0, 384, 128, False),
)
PIECE_BANKS = (0, 7, 1, 2, 3, 4)
LATER_PIECES = ((1, 0, 256, 0), (1, 256, 256, 3), (0, 0, 512, 4))
WEIGHT_BANKS = (0, 5, 2, 6)
GATE_BANK = 4


def tile_picked_grand_none_e_kernel(
    tc, xT, w1_words, w1_scales, gate, offs, cen, pos1, pos2, pos3, out
):
    nc = tc.nc
    with ExitStack() as ctx:
        keep = ctx.enter_context(tc.tile_pool(name="keep", bufs=1))
        psum = ctx.enter_context(tc.psum_pool(name="psum", bufs=1))

        def bank(number):
            return psum.tile([P, V], F32, name="bank", tag="bank%d" % number)

        offs_sb = keep.tile([P, S // LIST], U16, name="offs_sb")
        lists = [keep.tile([P, V // LIST], U16, name="list%d" % i) for i in range(D + 1)]

        w_scale = keep.tile([P, N], U8, name="w_scale", align_bytes=64)
        gate_rows = keep.tile([P, P], F32, name="gate_rows")
        ident = keep.tile([P, P], F32, name="ident")
        nc.vector.memset(gate_rows[:], 0.0)
        nc.vector.memset(w_scale[:].bitcast(I32), 0)
        make_identity(nc, ident[:])

        rows = xT.rearrange("(p j) t -> p j t", j=PACK)
        planes = [
            keep.tile([P, T], F32, name="plane%d" % j, tag="plane%d" % j, align_bytes=64) for j in range(PACK)
        ]
        nc.sync.dma_start(out=planes[0][:], in_=rows[:, 0, :])
        nc.sync.dma_start(offs_sb[:], offs)
        gate_runs = gate.rearrange("d r (t p) -> (d r t) p", p=P)
        stride = P + 1
        nc.sync.dma_start(out=gate_rows[0 : D * VT, :], in_=gate_runs[0 : (D * VT - 1) * stride + 1 : stride, :])
        for j in range(1, PACK):
            nc.sync.dma_start(out=planes[j][:], in_=rows[:, j, :])
        last_plane = planes[PACK - 1]
        w_codes = keep.tile([P, 2 * N], U8, name="w_codes", align_bytes=64)
        nc.sync.dma_start(out=w_codes[:], in_=w1_words[0])
        for q in range(4):
            nc.sync.dma_start(
                out=w_scale[32 * q : 32 * q + 4, :].bitcast(I32), in_=w1_scales[0, 4 * q : 4 * q + 4, :].bitcast(I32)
            )
        for list_sb, src in zip(lists, (cen, pos1, pos2, pos3)):
            nc.sync.dma_start(list_sb[:], src)

        gate_turned = bank(GATE_BANK)
        nc.tensor.transpose(gate_turned[:, 0:P], gate_rows[:], ident[:])
        weight = keep.tile([P, (D + 1) * VT], F32, name="weight")
        gate_sum = keep.tile([P, VT], F32, name="gate_sum")
        nc.vector.tensor_copy(out=weight[:, VT:], in_=gate_turned[:, 0 : D * VT])
        nc.vector.tensor_reduce(
            out=gate_sum[:],
            in_=gate_turned[:, 0 : D * VT].rearrange("p (d t) -> p t d", d=D),
            axis=mybir.AxisListType.X,
            op=ADD,
        )
        nc.vector.tensor_scalar(out=weight[:, 0:VT], in0=gate_sum[:], scalar1=-1.0, scalar2=1.0, op0=MULT, op1=ADD)

        weight_bank = []
        weight_row = {}
        for d, kept in enumerate((ALL, BACK, ALL, LOW)):
            spread = bank(WEIGHT_BANKS[d])
            for t in range(VT):
                col = d * VT + t
                nc.tensor.transpose(
                    spread[:, t * P : (t + 1) * P], weight[:, col : col + 1].to_broadcast([P, P]), ident[:]
                )
            weight_bank.append(spread)
            weight_row[d] = keep.tile([P, kept.stop], F32, name="weight_row%d" % d)
            nc.scalar.activation(out=weight_row[d][:, kept], in_=spread[:, kept], func=COPY)

        grouped = [keep.tile([P, HALF, PACK], BF16, name="grouped%d" % h, align_bytes=64) for h in range(2)]
        half_offs = [offs_sb[:, h * HALF // LIST : (h + 1) * HALF // LIST] for h in range(2)]
        for j in range(PACK - 1):
            for h in range(2):
                nc.vector.tensor_copy(out=grouped[h][:, :, j], in_=planes[j][:].indirect(half_offs[h]))
        dense_g = keep.tile([P, QUARTER], BF16, name="dense_g", tag="plane%d" % (PACK - 2), align_bytes=64)
        dense_s = keep.tile([P, QUARTER], BF16, name="dense_s")
        nc.vector.tensor_copy(out=grouped[1][:, :, PACK - 1], in_=last_plane[:].indirect(half_offs[1]))
        for first, count in LAID_BY_GPSIMD:
            nc.scalar.activation(
                out=dense_g[:, first : first + count],
                in_=last_plane[:].indirect(offs_sb[:, first // LIST : (first + count) // LIST]),
                func=COPY,
            )
            nc.gpsimd.tensor_copy(
                out=grouped[0][:, first : first + count, PACK - 1], in_=dense_g[:, first : first + count]
            )
        nc.scalar.activation(
            out=dense_s[:], in_=last_plane[:].indirect(offs_sb[:, QUARTER // LIST : HALF // LIST]), func=COPY
        )
        for first, count in LAID_BY_SCALAR:
            nc.scalar.copy(
                out=grouped[0][:, first : first + count, PACK - 1],
                in_=dense_s[:, first - QUARTER : first - QUARTER + count],
            )

        codes = [
            keep.tile([P, HALF], U32, name="codes0", align_bytes=64),
            keep.tile([P, HALF], U32, name="codes1", tag="plane%d" % (PACK - 2), align_bytes=64),
        ]
        scales = [keep.tile([P, HALF], U8, name="scales%d" % h, align_bytes=64) for h in range(2)]
        y = [keep.tile([P, S], F32, name="y%d" % b) for b in range(2)]

        def product(b, h, first, count, on_vector, number):
            acc = bank(number)
            nc.tensor.matmul_mx(
                out=acc[:, 0:count],
                lhsT=w_codes[:, 2 * P * b : 2 * P * (b + 1)].bitcast(FP4X4),
                lhsT_scale=w_scale[:, P * b : P * (b + 1)],
                rhs=codes[h][:, first : first + count].bitcast(FP8X4),
                rhs_scale=scales[h][:, first : first + count],
                start=True,
                stop=True,
            )
            dst = y[b][:, h * HALF + first : h * HALF + first + count]
            if on_vector:
                nc.vector.tensor_copy(out=dst, in_=acc[:, 0:count])
            else:
                nc.scalar.activation(out=dst, in_=acc[:, 0:count], func=COPY)

        for number, (h, first, count, on_vector) in zip(PIECE_BANKS, PIECES):
            flat = grouped[h][:].rearrange("p n j -> p (n j)")
            nc.vector.quantize_mx(
                out=codes[h][:, first : first + count].bitcast(FP8X4),
                scales=scales[h][:, first : first + count],
                in_=flat[:, PACK * first : PACK * (first + count)],
            )
            product(0, h, first, count, on_vector, number)
        for h, first, count, number in LATER_PIECES:
            product(1, h, first, count, False, number)

        sums = {(b, cols.start): bank(2 * b + cols.start // SPAN) for b in range(2) for cols in (LOW, HIGH)}
        result = [keep.tile([P, V], F32, name="result%d" % b) for b in range(2)]

        def wide_tile(name):
            return keep.tile([P, V], F32, name=name)

        def look_up(b, d, cols):
            return y[b][:].indirect(lists[d][:, cols.start // LIST : cols.stop // LIST])

        def add_turned(b, d, term, cols):
            for first in range(cols.start, cols.stop, P):
                at = first % SPAN
                nc.tensor.matmul(
                    sums[b, first - at][:, at : at + P],
                    lhsT=term[:, first : first + P],
                    rhs=ident[:],
                    is_transpose=True,
                    start=d == ADDED[0] and at == 0,
                    stop=d == ADDED[-1] and at == SPAN - P,
                )

        def fused(b, d, term, cols):
            nc.vector.tensor_tensor(out=term[:, cols], in0=look_up(b, d, cols), in1=weight_row[d][:, cols], op=MULT)
            add_turned(b, d, term, cols)

        def fetch(b, d):
            plain = wide_tile("plain%d%d" % (b, d))
            nc.scalar.activation(out=plain[:], in_=look_up(b, d, ALL), func=COPY)
            return plain

        def weigh(d, dst, plain, cols):
            nc.vector.tensor_tensor(out=dst, in0=plain[:, cols], in1=weight_bank[d][:, cols], op=MULT)

        def copy_out(b, cols, staged):
            nc.scalar.activation(out=staged, in_=sums[b, cols.start][:, 0:SPAN], func=COPY)

        def turn(b, cols, staged):
            total = sums[b, cols.start]
            for at in range(0, SPAN, P):
                nc.tensor.transpose(total[:, SPAN + at : SPAN + at + P], staged[:, at : at + P], ident[:])

        def turn_back(b, cols):
            staged = keep.tile([P, SPAN], F32, name="staged%d_%d" % (b, cols.start))
            copy_out(b, cols, staged[:])
            turn(b, cols, staged[:])

        def finish(b, closing, cols):
            nc.vector.tensor_tensor(
                out=result[b][:, cols], in0=sums[b, cols.start][:, SPAN:V], in1=closing, op=ADD
            )
            nc.sync.dma_start(out=out[b * P : (b + 1) * P, cols], in_=result[b][:, cols])

        term = {(b, d): wide_tile("term%d%d" % (b, d)) for b in range(2) for d in ADDED}

        fused(0, 0, term[0, 0], ALL)
        plain01 = fetch(0, 1)
        fused(0, 2, term[0, 2], ALL)
        weigh(1, term[0, 1][:, FRONT], plain01, FRONT)
        nc.gpsimd.tensor_tensor(out=term[0, 1][:, BACK], in0=plain01[:, BACK], in1=weight_row[1][:, BACK], op=MULT)
        add_turned(0, 1, term[0, 1], ALL)
        plain03 = fetch(0, CLOSING)

        fused(1, 0, term[1, 0], ALL)
        plain11 = fetch(1, 1)
        closing1 = wide_tile("closing1")
        copy_out(0, LOW, closing1[:, LOW])
        fused(1, 2, term[1, 2], LOW)
        turn(0, LOW, closing1[:, LOW])
        fused(1, 2, term[1, 2], HIGH)
        closing0_low = weight_row[2][:, LOW]
        nc.gpsimd.tensor_tensor(out=closing0_low, in0=plain03[:, LOW], in1=weight_row[CLOSING][:, LOW], op=MULT)
        for cols in (LOW, HIGH):
            weigh(1, term[1, 1][:, cols], plain11, cols)
            add_turned(1, 1, term[1, 1], cols)

        plain13 = fetch(1, CLOSING)
        nc.vector.tensor_copy(out=plain11[:, LOW], in_=sums[0, HIGH.start][:, 0:SPAN])
        turn(0, HIGH, plain11[:, LOW])
        closing0_high = plain11[:, HIGH]
        weigh(CLOSING, closing0_high, plain03, HIGH)
        for cols in (LOW, HIGH):
            turn_back(1, cols)
        finish(0, closing0_low, LOW)
        weigh(CLOSING, closing1[:], plain13, ALL)
        finish(0, closing0_high, HIGH)
        for cols in (LOW, HIGH):
            finish(1, closing1[:, cols], cols)
